import numpy as np, ml_dtypes
CORES = [1,5,17,21,33,37,49,53]
N = 8
BF = ml_dtypes.bfloat16
W, C, S, RO, B = 4096, 128, 3, 3, 32
def parts(rng):
    x = rng.integers(122, 135, (N, 8, 16, W), dtype=np.int16)
    far = rng.random((N, 8, 16, W), dtype=np.float32) < rng.choice(np.array([0.02, 0.06, 0.1]), (N, 8, 16, 1))
    far = far | (rng.random((N, 8, 1, W)) < 0.02)
    x = np.where(far, rng.integers(0, 256, (N, 8, 16, W), dtype=np.int16), x)
    return x, rng.integers(0, W, (N, 8, 16, C)), rng.integers(0, 4096, (N, 8, 16, 1)), rng.integers(-160, 161, (N, 8, RO, S, C))
def pack(x, c, w, sl):
    return {"xt": np.ascontiguousarray(np.reshape(x, (N, 128, W))).astype(np.float32).astype(BF), "ch": np.ascontiguousarray(np.reshape(c, (N, 128, C))).astype(np.int32),
            "wt": np.ascontiguousarray(np.reshape(w, (N, 128, 1))).astype(np.int32), "sl": np.ascontiguousarray(np.reshape(sl, (N, 8, RO * S * C))).astype(np.int32)}
def setup_inputs(rng):
    return pack(*parts(rng))
def setup_inputs_spread(rng):
    x = np.minimum((np.exp2(8 * rng.random((N, 8, 1, W))) * rng.random((N, 8, 16, W), dtype=np.float32)).astype(np.int16), 255)
    x = np.where(rng.random((N, 8, 16, 1)) < 0.4, 255 - x, x)
    c = np.minimum((W * rng.random((N, 8, 16, C)) ** rng.choice(np.array([0.25, 1.0, 3.0]), (N, 8, 1, C))).astype(np.int64), W - 1)
    w = np.minimum(np.exp2(12 * rng.random((N, 8, 16, 1))).astype(np.int64) - 1, 4095)
    return pack(x, c, w, rng.integers(-255, 256, (N, 8, RO, S, C)))
def setup_inputs_ends(rng):
    b = np.zeros((N, 8, 16, W), bool); sh = int(rng.integers(0, 4))
    for r in range(N):
        for g in range(8):
            md = 4 if g == 7 else (g + r + sh) % 4
            if md == 0: b[r, g] = rng.random((1, W)) < 0.042
            elif md == 1: b[r, g] = rng.random((16, W)) < rng.choice(np.array([0.042, 0.5, 0.958]), (16, 1))
            elif md == 2: b[r, g] = rng.random((1, W)) < 0.958
            elif md == 3: b[r, g] = rng.random((16, W)) < 0.042
            else:
                b[r, g] = rng.random((1, W)) < 0.042; b[r, g, 15] = rng.random(W) < 0.042
    b[:, 7, :, 0] = False; b[:, 7, :, W - 1] = True
    c = np.where(rng.random((N, 8, 16, C)) < rng.choice(np.array([0.0, 0.0625, 0.5, 0.5, 0.9375, 1.0]), (N, 8, 1, C)), W - 1, 0)
    c[:, :, :, 0] = 0; c[:, 7, :, C - 2] = W - 1
    k = np.arange(16); nm = np.where(k % 2 == 0, W - 1, 0); nx = (((nm * 16) >> 6) + nm + 613 * k) & (W - 1)
    c[:, 7, :, C - 1] = nm
    last, first = b[N - 1, 7], b[0, 7]
    last[:, nx] = False; last[:15, nx[0]] = True; last[15, nx] = True
    first[:, nx] = False; first[:, nx[0]] = True
    w = 4095 * rng.integers(0, 2, (N, 8, 16, 1)); w[:, 1, 0] = 0; w[:, 1, 1] = 4095; w[0, 0] = 0; w[N - 1, 7] = 4095
    sl = 510 * rng.integers(0, 2, (N, 8, RO, S, C)) - 255; sl[N - 1, 7, 0, 0, C - 1] = -255
    return pack(255 * b.astype(np.int16), c, w, sl)
def setup_inputs_corners(rng):
    x, c, w, sl = parts(rng); i = np.arange(C)
    x[1, 0] = 255 * rng.integers(0, 2, (16, W))
    pin = 5 * C + int(rng.integers(0, C)) if W == 4096 else -1
    for a, m in ((0, int(rng.choice(np.array([31, 32, 33, 8 * C - 1])))), (2, 8 * C)):
        x[a] = rng.integers(0, 256, (8, 16, 1)); x[a, 7, 15] = 255; x[a, 7, 14] = 0
        ways = np.stack([np.zeros((8, C), np.int64), np.full((8, C), W - 1), np.tile(B * i, (8, 1)), np.tile(B * i + B - 1, (8, 1)), rng.integers(0, W, (8, C))])
        c[a] = np.take_along_axis(ways, rng.integers(0, 5, (1, 8, C)), 0).reshape(8, 1, C)
        o = rng.permutation(8 * C)
        if a == 0: o = o[o != pin]
        h = np.zeros(8 * C, bool); h[o[:m]] = True
        sl[a, :, 0] = -255; sl[a, :, 0, 0] = np.where(h.reshape(8, C), 0, -255)
    if N > 4: x[4, :4] = rng.integers(0, 256, (4, 16, 1))
    c[1, 5] = 0; c[1, 6] = W - 1
    for a in (1, 3):
        sl[a] = rng.choice(np.array([-255, -1, 0, 1, 255]), (8, RO, S, C))
        c[a, :5] = np.where(rng.random((5, 1, C)) < 0.5, B * i + (B - 1) * rng.integers(0, 2, (5, 16, C)), c[a, :5])
    w[:, 1] = 0; w[:, 2] = 4095; w[:, 3, :15] = 0; w[:, 3, 15] = 4095; w[:, 4] = 1
    for g, low in ((0, 0), (6, 4095)):
        v = rng.integers(220, 256, 16); v[14] = 2; v[15] = 1
        z = rng.integers(3500, 4096, 16); z[14] = rng.integers(0, 2048); z[15] = 0
        z[15] = (low - int(np.sum(v * z))) & 4095
        if (int(np.sum(v * z)) >> 12) & 1 == 0: z[14] += 2048
        x[0, g] = v.reshape(16, 1); w[0, g] = z.reshape(16, 1)
    if pin >= 0:
        p = int(rng.integers(0, 16)); x[0, 5, p] = 1; w[0, 5] = 0; w[0, 5, p] = 4075
        first = (((c[0, 5] * 4075) >> 6) + c[0, 5]) & (W - 1)
        c[0, 5] = np.where(first == 2557, 0, c[0, 5]); c[0, 5, :, pin - 5 * C] = 4093; sl[0, 5, 0, 0, pin - 5 * C] = 0
        nx = (2557 + 613 * np.arange(16)) & (W - 1); own = x[1, 5]; own[:, nx] = rng.integers(122, 135, (16, 1))
    return pack(x, c, w, sl)
def setup_inputs_ties(rng):
    x = rng.integers(0, 254, (N, 8, 16, 1), dtype=np.int16) + 2 * (rng.random((N, 8, 16, W), dtype=np.float32) < rng.choice(np.array([0.02, 0.05]), (N, 8, 16, 1))).astype(np.int16)
    c = rng.integers(0, W, (N, 8, 16, C)); few = np.take_along_axis(c, rng.integers(0, 4, (N, 8, 16, C)), 2)
    c = np.where(rng.random((N, 8, 1, C)) < 0.5, few, c); sl = rng.integers(-3, 4, (N, 8, RO, S, C))
    x[0] = rng.integers(0, 256, (8, 16, 1)); x[2, :2] = rng.integers(0, 256, (2, 16, 1)); c[0] = rng.integers(0, W, (8, 1, C))
    x[1, :, 15] = rng.integers(0, 254, (8, 1)) + 2 * (np.arange(W) & 1)
    h = np.zeros(8 * C, bool); h[rng.permutation(8 * C)[:26 + 2 * int(rng.integers(0, 3)) + 32 * int(rng.integers(0, C // 4))]] = True
    sl[0, :, 0] = -1; sl[0, :, 0, 0] = np.where(h.reshape(8, C), 0, -1)
    return pack(x, c, rng.integers(0, 4096, (N, 8, 16, 1)), sl)
def check_inputs(d):
    bad = []
    for k, lo, hi in (("xt", 0, 255), ("ch", 0, W - 1), ("wt", 0, 4095), ("sl", -255, 255)):
        v = np.asarray(d[k]).astype(np.float64)
        if not (np.min(v) >= lo and np.max(v) <= hi): bad.append("range of " + k)
        if not np.all(v == np.floor(v)): bad.append("whole numbers in " + k)
    return bad
def look(tab, c):
    v = np.take_along_axis(tab, c.reshape(8, 1, 16 * C), 2).reshape(8, 16, 16, C)
    y = np.max(v, axis=2).astype(np.int64); m = np.min(v, axis=2).astype(np.int64)
    return y, np.add.reduce(y - m, axis=1)
def reference(xt, ch, wt, sl):
    X = xt.astype(np.float32).astype(np.int32).reshape(N, 8, 16, W); c = ch.astype(np.int64).reshape(N, 8, 16, C)
    w = wt.astype(np.int64).reshape(N, 8, 16, 1); slack = sl.astype(np.int64).reshape(N, 8, RO, S, C)
    kappa = np.zeros(N, np.int64); k613 = (613 * np.arange(16)).reshape(1, 16, 1)
    for t in range(RO):
        states, tops, wrong = [], [], []
        for r in range(N):
            q = (r + 1 + t % (N - 1)) % N
            s = c[r]; y, e = look(X[r], s); eq = look(X[q], s)[1]
            fs, fy = s, y; right = np.ones((8, C), bool)
            for j in range(S):
                u = np.add.reduce(w[r] * y, axis=1) & 4095
                n = (((s * u[:, None, :]) >> 6) + s + k613 + 77 * j + kappa[r]) & (W - 1)
                yn, en = look(X[r], n); qn = look(X[q], n)[1]; a = slack[r, :, t, j]
                guess = en <= e + a; true = en + qn <= e + eq + a
                go = (right & true)[:, None, :]; fs = np.where(go, n, fs); fy = np.where(go, yn, fy)
                right = right & (guess == true)
                on = guess[:, None, :]; s = np.where(on, n, s); y = np.where(on, yn, y); e = np.where(guess, en, e); eq = np.where(guess, qn, eq)
            states.append(fs); tops.append(fy); wrong.append(np.count_nonzero(~right) & 31)
        for r in range(N):
            place = (B * np.arange(C)[None, :] + (np.add.reduce(w[r] * tops[r], axis=1) & (B - 1)))[:, None, :]
            old = np.take_along_axis(X[r], place, 2)
            np.put_along_axis(X[r], place, ((old + tops[r]) >> 1).astype(np.int32), 2)
        c = np.stack(states); kappa = np.array(wrong, np.int64)
    return {"yc": c.reshape(N, 128, C).astype(np.float32), "yx": X.reshape(N, 128, W).astype(np.float32).astype(BF)}

@@ -1,0 +1,440 @@
+from concourse.mybir import AluOpType, AxisListType, ActivationFunctionType
+
+RO, NL = 3, 4
+SCRATCH = {
+    "tab": ("sbuf", [128, 4096], "bfloat16"),
+    "nW": ("sbuf", [128, 512], "int32"),
+    "L": ("sbuf", [128, RO * NL * 128], "uint16"),
+    "Lr": ("sbuf", [128, RO * NL * 128], "uint16"),
+    "gA0": ("sbuf", [128, 2048], "bfloat16"),
+    "gA1": ("sbuf", [128, 2048], "bfloat16"),
+    "gS0": ("sbuf", [128, 2048], "bfloat16"),
+    "gS1": ("sbuf", [128, 2048], "bfloat16"),
+    "Y": ("sbuf", [128, 8192], "bfloat16"),
+    "Mn": ("sbuf", [128, 8192], "bfloat16"),
+    "YS": ("sbuf", [128, 2048], "bfloat16"),
+    "MS": ("sbuf", [128, 2048], "bfloat16"),
+    "Er": ("sbuf", [128, RO * NL * 8], "float32"),
+    "Eq": ("sbuf", [128, RO * NL * 8], "float32"),
+    "mx": ("sbuf", [128, 2048], "bfloat16"),
+    "mn": ("sbuf", [128, 2048], "bfloat16"),
+    "kp1": ("sbuf", [128, 128], "float32"),
+    "kp2": ("sbuf", [128, 128], "float32"),
+    "BK1": ("sbuf", [128, 128], "float32"),
+    "BKb": ("sbuf", [128, 128], "bfloat16"),
+    "Bp": ("sbuf", [128, 128], "bfloat16"),
+    "Bn": ("sbuf", [128, 128], "bfloat16"),
+    "Wh": ("sbuf", [128, 128], "bfloat16"),
+    "Wl": ("sbuf", [128, 128], "bfloat16"),
+    "ones": ("sbuf", [128, 128], "bfloat16"),
+    "Bk": ("sbuf", [128, 2048], "bfloat16"),
+    "Bnk": ("sbuf", [128, 2048], "bfloat16"),
+    "Wk": ("sbuf", [128, 2048], "bfloat16"),
+    "slz": ("sbuf", [128, 1152], "int32"),
+    "slb": ("sbuf", [128, 1152], "bfloat16"),
+    "a8": ("sbuf", [128, 144], "float32"),
+    "wI": ("sbuf", [128, 1], "int32"),
+    "wq": ("sbuf", [128, 4], "int32"),
+    "wf": ("sbuf", [128, 4], "float32"),
+    "kI": ("sbuf", [128, 4], "int32"),
+    "kf": ("sbuf", [128, 8], "float32"),
+    "cKi": ("sbuf", [128, 32], "int32"),
+    "cK": ("sbuf", [128, 32], "float32"),
+    "Ui": ("sbuf", [128, 128], "int32"),
+    "ua": ("sbuf", [128, 128], "int32"),
+    "P": ("sbuf", [128, 128], "float32"),
+    "P3": ("sbuf", [128, 128], "float32"),
+    "Qi": ("sbuf", [128, 128], "int32"),
+    "h": ("sbuf", [128, 128], "float32"),
+    "hd": ("sbuf", [128, 128], "float32"),
+    "thr": ("sbuf", [128, 128], "float32"),
+    "cat": ("sbuf", [128, 96], "float32"),
+    "dl": ("sbuf", [128, 64], "float32"),
+    "HD": ("sbuf", [128, 48], "float32"),
+    "rt": ("sbuf", [128, 64], "float32"),
+    "K": ("sbuf", [128, 32], "float32"),
+    "Ki": ("sbuf", [128, 64], "int32"),
+    "ci": ("sbuf", [128, 64], "int32"),
+    "cf": ("sbuf", [128, 64], "float32"),
+    "r3": ("sbuf", [128, 8], "bfloat16"),
+    "o1": ("sbuf", [128, 8], "uint16"),
+    "o2": ("sbuf", [128, 8], "uint16"),
+    "o3": ("sbuf", [128, 8], "uint16"),
+    "old": ("sbuf", [128, 128], "float32"),
+    "sm": ("sbuf", [128, 128], "int32"),
+    "sn": ("sbuf", [128, 128], "int32"),
+    "fin": ("sbuf", [128, 128], "float32"),
+    "pU": ("psum", [128, 512], "float32"),
+    "pE": ("psum", [128, 512], "float32"),
+    "pD": ("psum", [128, 512], "float32"),
+    "pV": ("psum", [128, 512], "float32"),
+    "pX": ("psum", [128, 512], "float32"),
+    "pY": ("psum", [128, 512], "float32"),
+    "pZ": ("psum", [128, 512], "float32"),
+    "pK": ("psum", [128, 512], "float32"),
+}
+PSUM = [n for n in SCRATCH if SCRATCH[n][0] == "psum"]
+SEMAPHORES = (["qv", "qs", "qp", "qg", "sent", "ld0", "ld1", "ld2", "ld3", "st0", "st1", "st2"]
+              + ["l%d" % i for i in range(RO * NL)] + ["e%d" % i for i in range(RO * NL)])
+
+ORDER = ("GA0a vGA0b K P0 MA0 U0 C0 GS0 GA1 mA0 E0 N0 P1 X0 MS0 mS0 F0 B0 "
+         "MA1 U1 mA1 E1 C1 GS1 GA2 D1 N1 P2 X1 R0 MS1 mS1 F1 B1 "
+         "MA2 U2 mA2 E2 C2 GS2 GA3 GS3a S X2 R1 MS2 mS2 F2 B2 vGS3b R2 "
+         "MS3 F3 mS3 B3 MA3 x3 R3 mA3 y3 J0 J1 J2 J3 Z")
+
+
+def rank_program(g, core, T, topo):
+    rank = T.rank_of(core)
+    if rank is None:
+        return
+    op = AluOpType
+    copy_fn = ActivationFunctionType.Copy
+    n_ranks = len(T.cores)
+    Q = {"g": g, "v": g.vector, "s": g.scalar, "p": g.tensor, "y": g.sync}
+    cnt = {"v": 0, "s": 0, "p": 0, "g": 0}
+    known = {"g": {}, "v": {}, "s": {}, "p": {}, "y": {}}
+    log = {}
+
+    def need(q, outs, ins):
+        evs = []
+        for buf, lo, hi, w in [(o[1], o[2], o[3], True) for o in outs] + [(i[1], i[2], i[3], False) for i in ins]:
+            for (lo2, hi2, w2, q2, s2, v2, c2) in log.get(buf, []):
+                if q2 == q:
+                    if not (w2 and (q != "p" or not w) and lo < hi2 and lo2 < hi):
+                        continue
+                elif buf in PSUM:
+                    pass
+                elif not ((w or w2) and lo < hi2 and lo2 < hi):
+                    continue
+                evs.append((s2, v2, c2))
+        best = {}
+        for s2, v2, c2 in evs:
+            if known[q].get(s2, 0) < v2 and (s2 not in best or best[s2][0] < v2):
+                best[s2] = (v2, c2)
+        for s2 in list(best):
+            if any(s3 != s2 and best[s3][1].get(s2, 0) >= best[s2][0] for s3 in best):
+                continue
+            v2, c2 = best[s2]
+            Q[q].wait_ge(T.sem[s2], v2)
+        for s2 in best:
+            v2, c2 = best[s2]
+            for s3 in c2:
+                known[q][s3] = max(known[q].get(s3, 0), c2[s3])
+            known[q][s2] = max(known[q].get(s2, 0), v2)
+
+    def note(q, outs, ins, s, v, clock):
+        for o in outs:
+            log[o[1]] = [a for a in log.get(o[1], []) if not (o[2] <= a[0] and a[1] <= o[3])]
+            log[o[1]].append((o[2], o[3], True, q, s, v, clock))
+        for i in ins:
+            log.setdefault(i[1], [])
+            log[i[1]] = [a for a in log[i[1]] if a[2] or a[3] != q or not (i[2] <= a[0] and a[1] <= i[3])]
+            log[i[1]].append((i[2], i[3], False, q, s, v, clock))
+
+    def run(q, call, outs, ins):
+        need(q, outs, ins)
+        cnt[q] += 1
+        call().then_inc(T.sem["q" + q], 1)
+        clock = dict(known[q])
+        clock["q" + q] = cnt[q]
+        note(q, outs, ins, "q" + q, cnt[q], clock)
+
+    def dma(q, out, in_, s):
+        o = [out] if out[1] else []
+        i = [in_] if in_[1] else []
+        need(q, o, i)
+        Q[q].dma_start(out[0], in_[0]).then_inc(T.sem[s], 16)
+        note("dma", o, i, s, 16, dict(known[q]))
+
+    def ext(ap):
+        return (ap, None, 0, 0)
+
+    def A(name, lo=0, hi=None, st=1):
+        if hi is None:
+            hi = SCRATCH[name][1][1]
+        t = T[name]
+        return (t[:, lo:hi] if st == 1 else t[:, lo:hi:st], name, lo, hi)
+
+    def cp(out, in_):
+        run("v", lambda: g.vector.tensor_copy(out[0], in_[0]), [out], [in_])
+
+    def tt(out, a, b, o):
+        run("v", lambda: g.vector.tensor_tensor(out[0], a[0], b[0], o), [out], [a, b])
+
+    def ts(out, a, s1, s2, o1, o2=None):
+        ins = [a] + [s for s in (s1, s2) if isinstance(s, tuple)]
+        x1 = s1[0] if isinstance(s1, tuple) else s1
+        x2 = s2[0] if isinstance(s2, tuple) else s2
+        if o2 is None:
+            run("v", lambda: g.vector.tensor_scalar(out[0], a[0], x1, None, o1), [out], ins)
+        else:
+            run("v", lambda: g.vector.tensor_scalar(out[0], a[0], x1, x2, o1, o2), [out], ins)
+
+    def fill(out, c):
+        run("v", lambda: g.vector.memset(out[0], c), [out], [])
+
+    def scan(out, d0, d1, o0, o1):
+        run("v", lambda: g.vector.tensor_tensor_scan(out[0], d0[0], d1[0], 0.0, o0, o1), [out], [d0, d1])
+
+    def vgather(out, win, off):
+        run("v", lambda: g.vector.tensor_copy(out[0], win[0].indirect(off[0])), [out], [win, off])
+
+    def sgather(out, win, off):
+        run("s", lambda: g.scalar.activation(out[0], win[0].indirect(off[0]), copy_fn), [out], [win, off])
+
+    def scp(out, in_, scale=1.0, bias=0.0):
+        ins = [in_] + ([scale] if isinstance(scale, tuple) else [])
+        x = scale[0] if isinstance(scale, tuple) else scale
+        run("s", lambda: g.scalar.activation(out[0], in_[0], copy_fn, bias=bias, scale=x), [out], ins)
+
+    def mm(out, pairs, first=True, last=True):
+        for n, (l, r) in enumerate(pairs):
+            st, sp = first and n == 0, last and n == len(pairs) - 1
+            run("p", lambda: g.tensor.matmul(out[0], l[0], r[0], st, sp), [out], [l, r])
+
+    n_eng = min(len(topo.engines(a, b)) for a in T.cores for b in T.cores if a != b)
+    sends = [0]
+
+    def send(dst, out, in_, s):
+        need("g", [], [in_])
+        rid, pid, _ = topo.addr(dst)
+        m = sum(1 << e for e in topo.engines(core, dst)[:n_eng])
+        g.remote_dma(out[0], in_[0], T.sem[s], T.sem.sent, pid, rid, m)
+        sends[0] += n_eng
+        note("x", [out], [], s, n_eng, {})
+
+    dma("y", A("nW", 0, 128), ext(T.ch[:, :]), "ld0")
+    dma("s", A("wI"), ext(T.wt[:, :]), "ld1")
+    dma("y", A("tab"), ext(T.xt[:, :]), "ld2")
+    fill(A("slz"), 0)
+    need("s", [("", "slz", 0, 1152)], [])
+    g.scalar.dma_start(T.slz[0:128:16, :], T.sl[:, :]).then_inc(T.sem.ld3, 16)
+    note("dma", [A("slz")], [], "ld3", 16, dict(known["s"]))
+    run("g", lambda: g.iota(T.kp1[:, :], [[0, 8], [1, 16]], 1, 0, allow_small_or_imprecise_dtypes=True), [A("kp1")], [])
+    run("g", lambda: g.iota(T.kI[:, 0:1], [[0, 1]], 0, 1), [A("kI", 0, 1)], [])
+    run("g", lambda: g.affine_select(T.kp2[:, :], T.kp1[:, :], [[-16, 8], [0, 16]], op.is_ge, 0.0, 0, 1), [A("kp2")], [A("kp1")])
+    run("g", lambda: g.affine_select(T.BK1[:, :], T.kp2[:, :], [[16, 8], [0, 16]], op.is_ge, 0.0, 15, -1), [A("BK1")], [A("kp2")])
+    run("g", lambda: g.iota(T.cKi[:, :], [[4096, 4], [512, 8]], 0, 0), [A("cKi")], [])
+    fill(A("mx"), 1.0)
+    fill(A("mx", 0, 2048, 16), 0.0)
+    cp(A("L", 0, 128), A("nW", 0, 128))
+
+    def send_list(t, c):
+        i = t * NL + c
+        q = T.cores[(rank + 1 + t % (n_ranks - 1)) % n_ranks]
+        send(q, A("Lr", i * 128, i * 128 + 128), A("L", i * 128, i * 128 + 128), "l%d" % i)
+
+    def send_reply(t, c):
+        i = t * NL + c
+        p = T.cores[(rank - 1 - t % (n_ranks - 1)) % n_ranks]
+        send(p, A("Eq", i * 8, i * 8 + 8), A("Er", i * 8, i * 8 + 8), "e%d" % i)
+
+    send_list(0, 0)
+    for n, m in ((0, 4032), (1, 63), (2, 31)):
+        ts(A("wq", n, n + 1), A("wI"), m, None, op.bitwise_and)
+    cp(A("wf", 0, 3), A("wq", 0, 3))
+    cp(A("BKb"), A("BK1"))
+    for k in range(16):
+        ts(A("Bk", k * 128, k * 128 + 128), A("BKb"), k + 1.0, None, op.is_equal)
+    scp(A("mn"), A("mx"), -512.0, 512.0)
+    scp(A("Wk"), A("Bk"), A("wf", 2, 3))
+    ts(A("Bp"), A("BK1"), 0.5, None, op.is_ge)
+    ts(A("Bn"), A("BK1"), 0.5, -1.0, op.is_ge, op.mult)
+    ts(A("Wh"), A("Bp"), A("wf", 0, 1), None, op.mult)
+    ts(A("Wl"), A("Bp"), A("wf", 1, 2), None, op.mult)
+    ts(A("kI", 1, 2), A("kI", 0, 1), 15, None, op.bitwise_and)
+    ts(A("kf", 0, 1), A("kI", 1, 2), 64.0 * 613, -1048576.0, op.mult, op.add)
+    ts(A("kf", 1, 2), A("kI", 1, 2), 32.0, None, op.mult)
+    cp(A("kf", 2, 3), A("kf", 0, 1))
+    ts(A("kf", 3, 4), A("kf", 0, 1), 64.0 * 77, None, op.add)
+    ts(A("cK"), A("cKi"), A("kf", 1, 2), None, op.add)
+    cp(A("slb"), A("slz"))
+    for k in range(16):
+        mm(A("pK", 0, 72), [(A("Bk", k * 128, k * 128 + 128), A("slb", k, 1152, 16))], k == 0, k == 15)
+    ts(A("Bnk"), A("Bk"), -1.0, None, op.mult)
+    fill(A("ones"), 1.0)
+
+    def yv(c):
+        return A("Y", c * 2048 + 15, c * 2048 + 2048, 16)
+
+    def mv(c):
+        return A("Mn", c * 2048 + 15, c * 2048 + 2048, 16)
+
+    def sl(t, j):
+        return A("slb", (t * 3 + j) * 128, (t * 3 + j) * 128 + 128)
+
+    px3, pu3 = A("pZ", 0, 8), A("pZ", 32, 40)
+
+    def half(x):
+        return {"": (0, 128), "a": (0, 64), "b": (64, 128)}[x]
+
+    def blk(name, k):
+        return A(name, k * 128, k * 128 + 128)
+
+    def piece(t, w):
+        onv = w[0] == "v"
+        w = w[1:] if onv else w
+        kind = w.rstrip("0123ab")
+        rest = w[len(kind):]
+        c = int(rest[0]) if rest else 0
+        lo, hi = half(rest[1:]) if rest else (0, 128)
+        i = t * NL + c
+        if kind in ("GA", "GS"):
+            own = kind == "GA"
+            out = A(("gA%d" if own else "gS%d") % (c % 2), lo * 16, hi * 16)
+            (vgather if onv else sgather)(out, A("tab"), A("L" if own else "Lr", i * 128 + lo, i * 128 + hi))
+        elif kind == "MA":
+            scan(A("Y", c * 2048, c * 2048 + 2048), A("mx"), A("gA%d" % (c % 2)), op.mult, op.max)
+        elif kind == "mA":
+            scan(A("Mn", c * 2048, c * 2048 + 2048), A("mn"), A("gA%d" % (c % 2)), op.max, op.min)
+        elif kind == "MS":
+            scan(A("YS", lo * 16, hi * 16), A("mx", lo * 16, hi * 16), A("gS%d" % (c % 2), lo * 16, hi * 16), op.mult, op.max)
+        elif kind == "mS":
+            scan(A("MS", lo * 16, hi * 16), A("mn", lo * 16, hi * 16), A("gS%d" % (c % 2), lo * 16, hi * 16), op.max, op.min)
+        elif kind == "U":
+            mm(A("pU", 0, 128), [(A("Wh"), yv(c)), (A("Wl"), yv(c))])
+        elif kind == "E":
+            mm(A("pE", 0, 128), [(A("Bp"), yv(c)), (A("Bn"), mv(c))] + ([(A("Bp"), sl(t, 0))] if c == 0 else []))
+        elif kind == "D":
+            mm(A("pD", 0, 128), [(A("Bp"), yv(1)), (A("Bn"), mv(1)), (A("Bn"), yv(0)), (A("Bp"), mv(0))])
+            mm(A("pD", 128, 256), [(A("Bp"), yv(0)), (A("Bn"), mv(0)), (A("Bp"), sl(t, 1))])
+        elif kind == "N":
+            if c == 0:
+                cp(A("thr"), A("pE", 0, 128))
+            else:
+                tt(A("hd"), A("pD", 0, 128), A("h"), op.mult)
+                tt(A("thr"), A("hd"), A("pD", 128, 256), op.add)
+        elif kind == "S":
+            for n in range(9 if t == 0 else 0):
+                for d in (0, 8):
+                    scp(A("a8", n * 16 + d, n * 16 + d + 8), A("pK", n * 8, n * 8 + 8))
+        elif kind == "K":
+            if t > 0:
+                cp(A("nW", 0, 128), A("L", i * 128, i * 128 + 128))
+                run("v", lambda: g.vector.tensor_reduce(T.cf[:, 32:33], T.pK[:, 80:88], AxisListType.X, op.add),
+                    [A("cf", 32, 33)], [A("pK", 80, 88)])
+                ts(A("ci", 32, 33), A("cf", 32, 33), -1.0, None, op.mult)
+                ts(A("ci", 33, 34), A("ci", 32, 33), 31, None, op.bitwise_and)
+                ts(A("kf", 2, 3), A("ci", 33, 34), 64.0, A("kf", 0, 1), op.mult, op.add)
+                ts(A("kf", 3, 4), A("kf", 2, 3), 64.0 * 77, None, op.add)
+        elif kind == "P":
+            s = A("nW", c * 128, c * 128 + 128)
+            if c == 0:
+                ts(A("pV", 128, 256), s, 64.0, A("kf", 2, 3), op.mult, op.add)
+            else:
+                ts(A("pV", 128, 256), s, 64.0, 64.0 * 77, op.mult, op.add)
+            cp(A("pV", 0, 128), s)
+        elif kind == "C":
+            cp(A("Ui"), A("pU", 0, 128))
+            ts(A("ua"), A("Ui"), 4095, None, op.bitwise_and)
+            tt(A("P"), A("ua"), A("pV", 0, 128), op.mult)
+            p3 = A("P")
+            if c > 0:
+                ts(A("pV", 256, 384), A("P"), A("kf", 1 + c, 2 + c), None, op.add)
+                tt(A("h"), A("pE", 0, 128), A("thr"), op.is_le)
+                p3 = A("P3")
+                tt(p3, A("pV", 256, 384), A("h"), op.mult)
+            tt(A("Qi"), p3, A("pV", 128, 256), op.add)
+            ts(A("nW", (c + 1) * 128, (c + 2) * 128), A("Qi"), 6, 4095, op.arith_shift_right, op.bitwise_and)
+            cp(A("L", (i + 1) * 128, (i + 2) * 128), A("nW", (c + 1) * 128, (c + 2) * 128))
+            send_list(t, c + 1)
+        elif kind in ("X", "x", "y"):
+            px = px3 if c == 3 else A("pX", 8 * c, 8 * c + 8)
+            pu = pu3 if c == 3 else A("pX", 32 + 8 * c, 40 + 8 * c)
+            ys = [A("Y", c * 2048 + 16 * k + 15, c * 2048 + 2048, 256) for k in range(16)]
+            ms = [A("Mn", c * 2048 + 16 * k + 15, c * 2048 + 2048, 256) for k in range(16)]
+            if kind != "y":
+                mm(pu, [(blk("Wk", k), ys[k]) for k in range(16)])
+                mm(px, [(blk("Bk", k), ys[k]) for k in range(16)], True, False)
+            if kind != "x":
+                mm(px, [(blk("Bnk", k), ms[k]) for k in range(16)], False, True)
+        elif kind == "F":
+            mm(A("pY", 8 * c, 8 * c + 8), [(blk("Bk", k), A("YS", 16 * k + 15, 2048, 256)) for k in range(16)], True, False)
+        elif kind == "B":
+            mm(A("pY", 8 * c, 8 * c + 8), [(blk("Bnk", k), A("MS", 16 * k + 15, 2048, 256)) for k in range(16)], False, True)
+        elif kind in ("R", "r"):
+            (cp if kind == "R" else scp)(A("Er", i * 8, i * 8 + 8), A("pY", 8 * c, 8 * c + 8))
+            send_reply(t, c)
+        elif kind == "J" and c < 2:
+            for n in ([0, 1] if c == 0 else [2]):
+                cp(A("cat", 16 * n, 16 * n + 8), A("pX", 8 * n, 8 * n + 8))
+                tt(A("cat", 16 * n + 8, 16 * n + 16), A("pX", 8 * n, 8 * n + 8), A("Eq", (t * NL + n) * 8, (t * NL + n) * 8 + 8), op.add)
+            st = A("cat", 0, 16) if c == 0 else A("cat", 48, 64)
+            tt(A("dl", 0, 16), A("cat", 16 * c + 16, 16 * c + 32), st, op.subtract)
+            j = t * 3 + c
+            tt(A("HD", 16 * c, 16 * c + 16), A("dl", 0, 16), A("a8", j * 16, j * 16 + 16), op.is_le)
+            for d in (0, 8):
+                tt(A("dl", 16 + d, 24 + d), A("dl", d, d + 8), A("HD", 16 * c, 16 * c + 8), op.mult)
+            tt(A("cat", 48 + 16 * c, 64 + 16 * c), st, A("dl", 16, 32), op.add)
+            tt(A("rt", 8 * c, 8 * c + 8), A("HD", 16 * c, 16 * c + 8), A("HD", 16 * c + 8, 16 * c + 16), op.is_equal)
+        elif kind == "J" and c == 2:
+            cp(A("Ki", 0, 24), A("pX", 32, 56))
+            ts(A("Ki", 32, 56), A("Ki", 0, 24), 31, None, op.bitwise_and)
+            tt(A("K", 0, 24), A("Ki", 32, 56), A("cK", 0, 24), op.add)
+            j = t * 3 + 2
+            tt(A("cat", 80, 96), A("cat", 64, 80), A("a8", j * 16, j * 16 + 16), op.add)
+            tt(A("rt", 16, 24), A("rt", 0, 8), A("rt", 8, 16), op.mult)
+            tt(A("rt", 24, 32), A("rt", 0, 8), A("HD", 24, 32), op.mult)
+            tt(A("cf", 0, 8), A("HD", 8, 16), A("K", 8, 16), op.mult)
+            tt(A("cf", 8, 16), A("rt", 24, 32), A("K", 16, 24), op.mult)
+            tt(A("cf", 16, 24), A("K", 0, 8), A("cf", 0, 8), op.max)
+            tt(A("cf", 24, 32), A("cf", 16, 24), A("cf", 8, 16), op.max)
+        elif kind == "J":
+            cp(A("Ki", 24, 32), pu3)
+            tt(A("rt", 32, 40), A("cat", 88, 96), px3, op.subtract)
+            ts(A("Ki", 56, 64), A("Ki", 24, 32), 31, None, op.bitwise_and)
+            tt(A("rt", 40, 48), px3, A("cat", 80, 88), op.is_le)
+            tt(A("K", 24, 32), A("Ki", 56, 64), A("cK", 24, 32), op.add)
+            tt(A("rt", 48, 56), A("rt", 16, 24), A("K", 24, 32), op.mult)
+        elif kind == "Z":
+            last = t == RO - 1
+            n = (t * NL + 3) * 8
+            tt(A("HD", 32, 40), A("Eq", n, n + 8), A("rt", 32, 40), op.is_le)
+            tt(A("HD", 40, 48), A("HD", 32, 40), A("rt", 48, 56), op.mult)
+            tt(A("ci", 0, 8), A("HD", 40, 48), A("cf", 24, 32), op.max)
+            ts(A("ci", 8, 16), A("ci", 0, 8), 5, None, op.arith_shift_right)
+            ts(A("ci", 16, 24), A("ci", 0, 8), 4095, None, op.bitwise_and)
+            if last:
+                cp(A("o3", 0, 4), A("ci", 16, 20))
+                ts(A("o3", 4, 8), A("ci", 20, 24), -2048.0, None, op.add)
+                sgather(A("old", 0, 64), A("tab", 0, 2048), A("o3", 0, 4))
+                sgather(A("old", 64, 128), A("tab", 2048, 4096), A("o3", 4, 8))
+                ts(A("o2"), A("ci", 8, 16), 16.0, 15.0, op.mult, op.add)
+            else:
+                cp(A("o1"), A("ci", 8, 16))
+                cp(A("o3"), A("ci", 16, 24))
+                sgather(A("old"), A("tab"), A("o3"))
+                vgather(A("L", (i_next(t)) * 128, (i_next(t)) * 128 + 128), A("nW"), A("o1"))
+                send_list(t + 1, 0)
+                ts(A("o2"), A("ci", 8, 16), 16.0, 15.0, op.mult, op.add)
+            parts = [(0, 64), (64, 128)] if last else [(0, 128)]
+            for a, b in parts:
+                yw, of = A("Y"), A("o2", a // 16, b // 16)
+                run("v", lambda: g.vector.tensor_tensor(T.sm[:, a:b], yw[0].indirect(of[0]), T.old[:, a:b], op.add),
+                    [A("sm", a, b)], [yw, of, A("old", a, b)])
+                ts(A("sn", a, b), A("sm", a, b), 1, None, op.arith_shift_right)
+                win, of3 = A("tab", 32 * a, 32 * b), A("o3", a // 16, b // 16)
+                run("v", lambda: g.vector.tensor_copy(win[0].indirect(of3[0]), T.sn[:, a:b]), [win], [A("sn", a, b), of3])
+                if last:
+                    dma("y" if a == 0 else "s", ext(T.yx[:, 32 * a:32 * b]), win, "st0" if a == 0 else "st1")
+            if last:
+                cp(A("o1"), A("ci", 8, 16))
+                vgather(A("fin"), A("nW"), A("o1"))
+                dma("y", ext(T.yc[:, :]), A("fin"), "st2")
+            else:
+                tt(A("rt", 56, 64), A("HD", 32, 40), A("rt", 40, 48), op.is_equal)
+                tt(A("r3"), A("rt", 56, 64), A("rt", 16, 24), op.mult)
+                mm(A("pK", 80, 88), [(A("ones"), A("r3"))])
+
+    def i_next(t):
+        return (t + 1) * NL
+
+    for t in range(RO):
+        for w in ORDER.split():
+            piece(t, w)
+
+    for q in "vspg":
+        g.wait_ge(T.sem["q" + q], cnt[q])
+    g.wait_ge(T.sem.sent, sends[0])
+    for s in ("ld0", "ld1", "ld2", "ld3", "st0", "st1", "st2"):
+        g.wait_ge(T.sem[s], 16)

@@ -1,86 +1,101 @@
-from concourse.mybir import AluOpType, AxisListType, ActivationFunctionType
+from concourse.mybir import AluOpType, ActivationFunctionType
 
 RO, NL = 3, 4
+BIG = 2.0 ** 25
+DG = 8192.0
 SCRATCH = {
     "tab": ("sbuf", [128, 4096], "bfloat16"),
-    "nW": ("sbuf", [128, 512], "int32"),
+    "chI": ("sbuf", [128, 128], "int32"),
+    "NW": ("sbuf", [128, 512], "int32"),
     "L": ("sbuf", [128, RO * NL * 128], "uint16"),
     "Lr": ("sbuf", [128, RO * NL * 128], "uint16"),
     "gA0": ("sbuf", [128, 2048], "bfloat16"),
     "gA1": ("sbuf", [128, 2048], "bfloat16"),
     "gS0": ("sbuf", [128, 2048], "bfloat16"),
     "gS1": ("sbuf", [128, 2048], "bfloat16"),
-    "Y": ("sbuf", [128, 8192], "bfloat16"),
-    "Mn": ("sbuf", [128, 8192], "bfloat16"),
-    "YS": ("sbuf", [128, 2048], "bfloat16"),
-    "MS": ("sbuf", [128, 2048], "bfloat16"),
-    "Er": ("sbuf", [128, RO * NL * 8], "float32"),
-    "Eq": ("sbuf", [128, RO * NL * 8], "float32"),
+    "YA": ("sbuf", [128, 8192], "bfloat16"),
+    "MA": ("sbuf", [128, 8192], "bfloat16"),
+    "YS": ("sbuf", [128, 8192], "bfloat16"),
+    "MS": ("sbuf", [128, 8192], "bfloat16"),
+    "Er": ("sbuf", [128, RO * 32], "float32"),
+    "Eq": ("sbuf", [128, RO * 32], "float32"),
     "mx": ("sbuf", [128, 2048], "bfloat16"),
     "mn": ("sbuf", [128, 2048], "bfloat16"),
-    "kp1": ("sbuf", [128, 128], "float32"),
-    "kp2": ("sbuf", [128, 128], "float32"),
-    "BK1": ("sbuf", [128, 128], "float32"),
-    "BKb": ("sbuf", [128, 128], "bfloat16"),
+    "rowb": ("sbuf", [128, 128], "float32"),
+    "rowj": ("sbuf", [128, 144], "float32"),
+    "rowx": ("sbuf", [128, 128], "float32"),
+    "dm": ("sbuf", [128, 128], "float32"),
+    "dt": ("sbuf", [128, 256], "float32"),
+    "dg": ("sbuf", [128, 128], "float32"),
     "Bp": ("sbuf", [128, 128], "bfloat16"),
     "Bn": ("sbuf", [128, 128], "bfloat16"),
+    "Bb": ("sbuf", [128, 128], "bfloat16"),
+    "Bbn": ("sbuf", [128, 128], "bfloat16"),
+    "Bh": ("sbuf", [128, 128], "bfloat16"),
+    "Bhn": ("sbuf", [128, 128], "bfloat16"),
+    "B8": ("sbuf", [128, 128], "bfloat16"),
     "Wh": ("sbuf", [128, 128], "bfloat16"),
     "Wl": ("sbuf", [128, 128], "bfloat16"),
-    "ones": ("sbuf", [128, 128], "bfloat16"),
-    "Bk": ("sbuf", [128, 2048], "bfloat16"),
-    "Bnk": ("sbuf", [128, 2048], "bfloat16"),
-    "Wk": ("sbuf", [128, 2048], "bfloat16"),
-    "slz": ("sbuf", [128, 1152], "int32"),
+    "Ip": ("sbuf", [128, 128], "bfloat16"),
+    "In": ("sbuf", [128, 128], "bfloat16"),
+    "neg": ("sbuf", [128, 128], "bfloat16"),
+    "c32": ("sbuf", [128, 128], "bfloat16"),
+    "sg": ("sbuf", [128, 128], "bfloat16"),
+    "hx": ("sbuf", [128, 128], "bfloat16"),
+    "Zp": ("sbuf", [128, 144], "bfloat16"),
+    "Zn": ("sbuf", [128, 144], "bfloat16"),
+    "Zw": ("sbuf", [128, 144], "bfloat16"),
+    "Z8": ("sbuf", [128, 144], "bfloat16"),
+    "slI": ("sbuf", [128, 1152], "int32"),
     "slb": ("sbuf", [128, 1152], "bfloat16"),
     "a8": ("sbuf", [128, 144], "float32"),
     "wI": ("sbuf", [128, 1], "int32"),
     "wq": ("sbuf", [128, 4], "int32"),
     "wf": ("sbuf", [128, 4], "float32"),
     "kI": ("sbuf", [128, 4], "int32"),
+    "pf": ("sbuf", [128, 4], "float32"),
     "kf": ("sbuf", [128, 8], "float32"),
-    "cKi": ("sbuf", [128, 32], "int32"),
+    "kq": ("sbuf", [128, 2], "int32"),
+    "cKi": ("sbuf", [128, 32], "float32"),
     "cK": ("sbuf", [128, 32], "float32"),
     "Ui": ("sbuf", [128, 128], "int32"),
     "ua": ("sbuf", [128, 128], "int32"),
     "P": ("sbuf", [128, 128], "float32"),
-    "P3": ("sbuf", [128, 128], "float32"),
+    "X": ("sbuf", [128, 128], "float32"),
     "Qi": ("sbuf", [128, 128], "int32"),
-    "h": ("sbuf", [128, 128], "float32"),
-    "hd": ("sbuf", [128, 128], "float32"),
-    "thr": ("sbuf", [128, 128], "float32"),
-    "cat": ("sbuf", [128, 96], "float32"),
-    "dl": ("sbuf", [128, 64], "float32"),
+    "cat": ("sbuf", [128, 48], "float32"),
+    "dl": ("sbuf", [128, 112], "float32"),
     "HD": ("sbuf", [128, 48], "float32"),
     "rt": ("sbuf", [128, 64], "float32"),
     "K": ("sbuf", [128, 32], "float32"),
     "Ki": ("sbuf", [128, 64], "int32"),
-    "ci": ("sbuf", [128, 64], "int32"),
-    "cf": ("sbuf", [128, 64], "float32"),
+    "ci": ("sbuf", [128, 32], "int32"),
+    "cf": ("sbuf", [128, 48], "float32"),
     "r3": ("sbuf", [128, 8], "bfloat16"),
-    "o1": ("sbuf", [128, 8], "uint16"),
+    "o13": ("sbuf", [128, 16], "uint16"),
     "o2": ("sbuf", [128, 8], "uint16"),
-    "o3": ("sbuf", [128, 8], "uint16"),
     "old": ("sbuf", [128, 128], "float32"),
     "sm": ("sbuf", [128, 128], "int32"),
     "sn": ("sbuf", [128, 128], "int32"),
     "fin": ("sbuf", [128, 128], "float32"),
     "pU": ("psum", [128, 512], "float32"),
-    "pE": ("psum", [128, 512], "float32"),
     "pD": ("psum", [128, 512], "float32"),
     "pV": ("psum", [128, 512], "float32"),
     "pX": ("psum", [128, 512], "float32"),
-    "pY": ("psum", [128, 512], "float32"),
+    "pC": ("psum", [128, 512], "float32"),
     "pZ": ("psum", [128, 512], "float32"),
-    "pK": ("psum", [128, 512], "float32"),
+    "pY": ("psum", [128, 512], "float32"),
+    "pW": ("psum", [128, 512], "float32"),
 }
 PSUM = [n for n in SCRATCH if SCRATCH[n][0] == "psum"]
 SEMAPHORES = (["qv", "qs", "qp", "qg", "sent", "ld0", "ld1", "ld2", "ld3", "st0", "st1", "st2"]
-              + ["l%d" % i for i in range(RO * NL)] + ["e%d" % i for i in range(RO * NL)])
+              + ["l%d%s" % (i, h) for i in range(RO * NL) for h in ("", "a", "b")]
+              + ["e%d%s" % (i, h) for i in range(RO * 2) for h in ("", "a", "b")])
 
-ORDER = ("GA0a vGA0b K P0 MA0 U0 C0 GS0 GA1 mA0 E0 N0 P1 X0 MS0 mS0 F0 B0 "
-         "MA1 U1 mA1 E1 C1 GS1 GA2 D1 N1 P2 X1 R0 MS1 mS1 F1 B1 "
-         "MA2 U2 mA2 E2 C2 GS2 GA3 GS3a S X2 R1 MS2 mS2 F2 B2 vGS3b R2 "
-         "MS3 F3 mS3 B3 MA3 x3 R3 mA3 y3 J0 J1 J2 J3 Z")
+ORDER = ("GA0a vGA0b K P0 YA0 U0 C0 GS0a GS0b GA1a GA1b MA0 e1 P1 YS0a MS0a YS0b MS0b "
+         "YA1a MA1a GS1a GS1b YA1b U1 MA1b D1 C1 H GA2a GA2b YS1a MS1a h e2 P2 YS1b MS1b "
+         "YA2a MA2a GS2a GS2b YA2b U2 MA2b D2 C2 GA3a GA3b X S YS2 MS2 F GS3a GS3b YA3a MA3a R YA3b x MA3b y "
+         "YS3a MS3a YS3b W MS3b w r J Jk Z")
 
 
 def rank_program(g, core, T, topo):
@@ -88,7 +103,7 @@ def rank_program(g, core, T, topo):
     if rank is None:
         return
     op = AluOpType
-    copy_fn = ActivationFunctionType.Copy
+    fn = ActivationFunctionType
     n_ranks = len(T.cores)
     Q = {"g": g, "v": g.vector, "s": g.scalar, "p": g.tensor, "y": g.sync}
     cnt = {"v": 0, "s": 0, "p": 0, "g": 0}
@@ -149,11 +164,18 @@ def rank_program(g, core, T, topo):
     def ext(ap):
         return (ap, None, 0, 0)
 
-    def A(name, lo=0, hi=None, st=1):
+    def A(name, lo=0, hi=None, st=1, rows=128):
         if hi is None:
             hi = SCRATCH[name][1][1]
         t = T[name]
-        return (t[:, lo:hi] if st == 1 else t[:, lo:hi:st], name, lo, hi)
+        return (t[0:rows, lo:hi] if st == 1 else t[0:rows, lo:hi:st], name, lo, hi)
+
+    def W(name, lo=0, hi=None):
+        hi = SCRATCH[name][1][1] if hi is None else hi
+        return (T[name][:, lo:hi], name, lo, hi)
+
+    def val(x):
+        return x[0] if isinstance(x, tuple) else x
 
     def cp(out, in_):
         run("v", lambda: g.vector.tensor_copy(out[0], in_[0]), [out], [in_])
@@ -161,14 +183,13 @@ def rank_program(g, core, T, topo):
     def tt(out, a, b, o):
         run("v", lambda: g.vector.tensor_tensor(out[0], a[0], b[0], o), [out], [a, b])
 
-    def ts(out, a, s1, s2, o1, o2=None):
-        ins = [a] + [s for s in (s1, s2) if isinstance(s, tuple)]
-        x1 = s1[0] if isinstance(s1, tuple) else s1
-        x2 = s2[0] if isinstance(s2, tuple) else s2
+    def ts(out, a, s1, s2, o1, o2=None, off=None):
+        ins = [a] + [s for s in (s1, s2, off) if isinstance(s, tuple)]
+        x = a[0] if off is None else a[0].indirect(off[0])
         if o2 is None:
-            run("v", lambda: g.vector.tensor_scalar(out[0], a[0], x1, None, o1), [out], ins)
+            run("v", lambda: g.vector.tensor_scalar(out[0], x, val(s1), None, o1), [out], ins)
         else:
-            run("v", lambda: g.vector.tensor_scalar(out[0], a[0], x1, x2, o1, o2), [out], ins)
+            run("v", lambda: g.vector.tensor_scalar(out[0], x, val(s1), val(s2), o1, o2), [out], ins)
 
     def fill(out, c):
         run("v", lambda: g.vector.memset(out[0], c), [out], [])
@@ -180,17 +201,20 @@ def rank_program(g, core, T, topo):
         run("v", lambda: g.vector.tensor_copy(out[0], win[0].indirect(off[0])), [out], [win, off])
 
     def sgather(out, win, off):
-        run("s", lambda: g.scalar.activation(out[0], win[0].indirect(off[0]), copy_fn), [out], [win, off])
+        run("s", lambda: g.scalar.activation(out[0], win[0].indirect(off[0]), fn.Copy), [out], [win, off])
 
-    def scp(out, in_, scale=1.0, bias=0.0):
+    def act(out, in_, scale=1.0, bias=0.0, f=None):
         ins = [in_] + ([scale] if isinstance(scale, tuple) else [])
-        x = scale[0] if isinstance(scale, tuple) else scale
-        run("s", lambda: g.scalar.activation(out[0], in_[0], copy_fn, bias=bias, scale=x), [out], ins)
+        run("s", lambda: g.scalar.activation(out[0], in_[0], f or fn.Copy, bias=bias, scale=val(scale)), [out], ins)
 
     def mm(out, pairs, first=True, last=True):
         for n, (l, r) in enumerate(pairs):
             st, sp = first and n == 0, last and n == len(pairs) - 1
             run("p", lambda: g.tensor.matmul(out[0], l[0], r[0], st, sp), [out], [l, r])
+
+    def iota(out, pattern, base, cm):
+        kw = {} if SCRATCH[out[1]][2] == "int32" else {"allow_small_or_imprecise_dtypes": True}
+        run("g", lambda: g.iota(out[0], pattern, base, cm, **kw), [out], [])
 
     n_eng = min(len(topo.engines(a, b)) for a in T.cores for b in T.cores if a != b)
     sends = [0]
@@ -203,73 +227,75 @@ def rank_program(g, core, T, topo):
         sends[0] += n_eng
         note("x", [out], [], s, n_eng, {})
 
-    dma("y", A("nW", 0, 128), ext(T.ch[:, :]), "ld0")
-    dma("s", A("wI"), ext(T.wt[:, :]), "ld1")
-    dma("y", A("tab"), ext(T.xt[:, :]), "ld2")
-    fill(A("slz"), 0)
-    need("s", [("", "slz", 0, 1152)], [])
-    g.scalar.dma_start(T.slz[0:128:16, :], T.sl[:, :]).then_inc(T.sem.ld3, 16)
-    note("dma", [A("slz")], [], "ld3", 16, dict(known["s"]))
-    run("g", lambda: g.iota(T.kp1[:, :], [[0, 8], [1, 16]], 1, 0, allow_small_or_imprecise_dtypes=True), [A("kp1")], [])
-    run("g", lambda: g.iota(T.kI[:, 0:1], [[0, 1]], 0, 1), [A("kI", 0, 1)], [])
-    run("g", lambda: g.affine_select(T.kp2[:, :], T.kp1[:, :], [[-16, 8], [0, 16]], op.is_ge, 0.0, 0, 1), [A("kp2")], [A("kp1")])
-    run("g", lambda: g.affine_select(T.BK1[:, :], T.kp2[:, :], [[16, 8], [0, 16]], op.is_ge, 0.0, 15, -1), [A("BK1")], [A("kp2")])
-    run("g", lambda: g.iota(T.cKi[:, :], [[4096, 4], [512, 8]], 0, 0), [A("cKi")], [])
-    fill(A("mx"), 1.0)
-    fill(A("mx", 0, 2048, 16), 0.0)
-    cp(A("L", 0, 128), A("nW", 0, 128))
-
-    def send_list(t, c):
-        i = t * NL + c
-        q = T.cores[(rank + 1 + t % (n_ranks - 1)) % n_ranks]
-        send(q, A("Lr", i * 128, i * 128 + 128), A("L", i * 128, i * 128 + 128), "l%d" % i)
-
-    def send_reply(t, c):
-        i = t * NL + c
-        p = T.cores[(rank - 1 - t % (n_ranks - 1)) % n_ranks]
-        send(p, A("Eq", i * 8, i * 8 + 8), A("Er", i * 8, i * 8 + 8), "e%d" % i)
-
-    send_list(0, 0)
-    for n, m in ((0, 4032), (1, 63), (2, 31)):
-        ts(A("wq", n, n + 1), A("wI"), m, None, op.bitwise_and)
-    cp(A("wf", 0, 3), A("wq", 0, 3))
-    cp(A("BKb"), A("BK1"))
-    for k in range(16):
-        ts(A("Bk", k * 128, k * 128 + 128), A("BKb"), k + 1.0, None, op.is_equal)
-    scp(A("mn"), A("mx"), -512.0, 512.0)
-    scp(A("Wk"), A("Bk"), A("wf", 2, 3))
-    ts(A("Bp"), A("BK1"), 0.5, None, op.is_ge)
-    ts(A("Bn"), A("BK1"), 0.5, -1.0, op.is_ge, op.mult)
-    ts(A("Wh"), A("Bp"), A("wf", 0, 1), None, op.mult)
-    ts(A("Wl"), A("Bp"), A("wf", 1, 2), None, op.mult)
-    ts(A("kI", 1, 2), A("kI", 0, 1), 15, None, op.bitwise_and)
-    ts(A("kf", 0, 1), A("kI", 1, 2), 64.0 * 613, -1048576.0, op.mult, op.add)
-    ts(A("kf", 1, 2), A("kI", 1, 2), 32.0, None, op.mult)
-    cp(A("kf", 2, 3), A("kf", 0, 1))
-    ts(A("kf", 3, 4), A("kf", 0, 1), 64.0 * 77, None, op.add)
-    ts(A("cK"), A("cKi"), A("kf", 1, 2), None, op.add)
-    cp(A("slb"), A("slz"))
-    for k in range(16):
-        mm(A("pK", 0, 72), [(A("Bk", k * 128, k * 128 + 128), A("slb", k, 1152, 16))], k == 0, k == 15)
-    ts(A("Bnk"), A("Bk"), -1.0, None, op.mult)
-    fill(A("ones"), 1.0)
-
-    def yv(c):
-        return A("Y", c * 2048 + 15, c * 2048 + 2048, 16)
-
-    def mv(c):
-        return A("Mn", c * 2048 + 15, c * 2048 + 2048, 16)
-
-    def sl(t, j):
-        return A("slb", (t * 3 + j) * 128, (t * 3 + j) * 128 + 128)
-
-    px3, pu3 = A("pZ", 0, 8), A("pZ", 32, 40)
-
     def half(x):
         return {"": (0, 128), "a": (0, 64), "b": (64, 128)}[x]
 
-    def blk(name, k):
-        return A(name, k * 128, k * 128 + 128)
+    def send_list(t, c, h=""):
+        i = t * NL + c
+        lo, hi = half(h)
+        q = T.cores[(rank + 1 + t % (n_ranks - 1)) % n_ranks]
+        send(q, W("Lr", i * 128 + lo, i * 128 + hi), W("L", i * 128 + lo, i * 128 + hi), "l%d%s" % (i, h))
+
+    def send_reply(t, lo, hi, s):
+        p = T.cores[(rank - 1 - t % (n_ranks - 1)) % n_ranks]
+        send(p, W("Eq", t * 32 + lo, t * 32 + hi), W("Er", t * 32 + lo, t * 32 + hi), s)
+
+    dma("y", W("chI"), ext(T.ch[:, :]), "ld0")
+    dma("s", W("wI"), ext(T.wt[:, :]), "ld1")
+    dma("y", W("tab"), ext(T.xt[:, :]), "ld2")
+    dma("s", A("slI", rows=8), ext(T.sl[:, :]), "ld3")
+    iota(A("kI", 0, 1), [[0, 1]], 0, 1)
+    iota(A("rowb"), [[16, 8], [0, 16]], 0, 0)
+    iota(A("rowj"), [[1, 144]], -15, 0)
+    iota(A("rowx"), [[0, 8], [1, 16]], 0, 0)
+    iota(A("cKi"), [[4096, 4], [512, 8]], 0, 0)
+    fill(A("mx"), 1.0)
+    fill(A("mx", 0, 2048, 16), 0.0)
+    act(A("mn"), A("mx"), -512.0, 512.0)
+    ts(A("kI", 1, 2), A("kI", 0, 1), 112, None, op.bitwise_and)
+    ts(A("kI", 2, 3), A("kI", 0, 1), 15, None, op.bitwise_and)
+    fill(A("neg"), -1.0)
+    cp(A("pf", 0, 3), A("kI", 0, 3))
+    ts(A("pf", 3, 4), A("kI", 0, 1), 16.0, None, op.mult)
+    fill(A("c32"), 1.0 / 32)
+    cp(A("L", 0, 128), A("chI"))
+    send_list(0, 0)
+    p_, blk_, k_, p16_ = [A("pf", n, n + 1) for n in range(4)]
+    ts(A("Bp"), A("rowb"), blk_, None, op.is_equal)
+    ts(A("Zp"), A("rowj"), blk_, None, op.is_equal)
+    ts(A("Ip"), A("rowj", 15, 143), p_, None, op.is_equal)
+    ts(A("Z8"), A("rowj"), p16_, None, op.is_equal)
+    ts(A("B8"), A("rowb"), p16_, BIG, op.is_equal, op.mult)
+    for n, m in ((0, 4032), (1, 63), (2, 31)):
+        ts(A("wq", n, n + 1), A("wI"), m, None, op.bitwise_and)
+    ts(A("kf", 4, 5), k_, 64.0 * 613, -1048576.0, op.mult, op.add)
+    cp(A("wf", 0, 3), A("wq", 0, 3))
+    for j in range(3):
+        ts(A("kf", j, j + 1), A("kf", 4, 5), 64.0 * 77 * j, None, op.add)
+    for j in (1, 2):
+        fill(A("kf", 4 + j, 5 + j), 64.0 * 77 * j)
+    for name, src, x in (("Wh", "Bp", A("wf", 0, 1)), ("Wl", "Bp", A("wf", 1, 2)), ("Bb", "Bp", BIG), ("Bbn", "Bp", -BIG),
+                         ("Bn", "Bp", -1.0), ("Bh", "Bp", BIG / 2), ("Bhn", "Bp", -BIG / 2), ("In", "Ip", -1.0),
+                         ("Zn", "Zp", -1.0), ("Zw", "Zp", A("wf", 2, 3))):
+        act(A(name), A(src), x)
+    ts(A("dt", 0, 128), A("rowx"), k_, -DG, op.is_lt, op.mult)
+    ts(A("dt", 128, 256), A("rowx"), k_, DG, op.is_equal, op.mult)
+    ts(A("wf", 3, 4), k_, 32.0, None, op.mult)
+    tt(A("dm"), A("dt", 0, 128), A("dt", 128, 256), op.add)
+    ts(A("cK"), A("cKi"), A("wf", 3, 4), None, op.add)
+    ts(A("dm", 15, 128, 16), A("dm", 15, 128, 16), -2 * DG, None, op.add)
+    cp(A("slb", rows=8), A("slI", rows=8))
+
+    def pick(name, k, rows=128):
+        return A(name, 15 - k, 143 - k, rows=rows)
+
+    mm(A("pX", 0, 72), [(pick("Z8", k, 8), A("slb", k, 1152, 16, rows=8)) for k in range(16)])
+
+    def ends(name, c, lo=0, hi=128):
+        return A(name, c * 2048 + 16 * lo + 15, c * 2048 + 16 * hi, 16)
+
+    def col(name, k, c0, c1):
+        return A(name, c0 * 2048 + 16 * k + 15, c1 * 2048, 256)
 
     def piece(t, w):
         onv = w[0] == "v"
@@ -277,157 +303,152 @@ def rank_program(g, core, T, topo):
         kind = w.rstrip("0123ab")
         rest = w[len(kind):]
         c = int(rest[0]) if rest else 0
-        lo, hi = half(rest[1:]) if rest else (0, 128)
+        h = rest[1:]
+        lo, hi = half(h)
         i = t * NL + c
+
+        def H(name, base=0, rows=128):
+            return A(name, base + lo, base + hi, rows=rows)
+
         if kind in ("GA", "GS"):
             own = kind == "GA"
-            out = A(("gA%d" if own else "gS%d") % (c % 2), lo * 16, hi * 16)
-            (vgather if onv else sgather)(out, A("tab"), A("L" if own else "Lr", i * 128 + lo, i * 128 + hi))
-        elif kind == "MA":
-            scan(A("Y", c * 2048, c * 2048 + 2048), A("mx"), A("gA%d" % (c % 2)), op.mult, op.max)
-        elif kind == "mA":
-            scan(A("Mn", c * 2048, c * 2048 + 2048), A("mn"), A("gA%d" % (c % 2)), op.max, op.min)
-        elif kind == "MS":
-            scan(A("YS", lo * 16, hi * 16), A("mx", lo * 16, hi * 16), A("gS%d" % (c % 2), lo * 16, hi * 16), op.mult, op.max)
-        elif kind == "mS":
-            scan(A("MS", lo * 16, hi * 16), A("mn", lo * 16, hi * 16), A("gS%d" % (c % 2), lo * 16, hi * 16), op.max, op.min)
-        elif kind == "U":
-            mm(A("pU", 0, 128), [(A("Wh"), yv(c)), (A("Wl"), yv(c))])
-        elif kind == "E":
-            mm(A("pE", 0, 128), [(A("Bp"), yv(c)), (A("Bn"), mv(c))] + ([(A("Bp"), sl(t, 0))] if c == 0 else []))
-        elif kind == "D":
-            mm(A("pD", 0, 128), [(A("Bp"), yv(1)), (A("Bn"), mv(1)), (A("Bn"), yv(0)), (A("Bp"), mv(0))])
-            mm(A("pD", 128, 256), [(A("Bp"), yv(0)), (A("Bn"), mv(0)), (A("Bp"), sl(t, 1))])
-        elif kind == "N":
-            if c == 0:
-                cp(A("thr"), A("pE", 0, 128))
+            out = W(("gA%d" if own else "gS%d") % (c % 2), lo * 16, hi * 16)
+            (vgather if onv else sgather)(out, W("tab"), W("L" if own else "Lr", i * 128 + lo, i * 128 + hi))
+        elif kind in ("YA", "YS", "MA", "MS"):
+            out, src = A(kind, c * 2048 + lo * 16, c * 2048 + hi * 16), A("g%s%d" % (kind[1], c % 2), lo * 16, hi * 16)
+            if kind[0] == "Y":
+                scan(out, A("mx", lo * 16, hi * 16), src, op.mult, op.max)
             else:
-                tt(A("hd"), A("pD", 0, 128), A("h"), op.mult)
-                tt(A("thr"), A("hd"), A("pD", 128, 256), op.add)
+                scan(out, A("mn", lo * 16, hi * 16), src, op.max, op.min)
+        elif kind == "U":
+            mm(H("pU"), [(A("Wh"), ends("YA", c, lo, hi)), (A("Wl"), ends("YA", c, lo, hi))])
+        elif kind == "e":
+            y0, m0 = ends("YA", 0, lo, hi), ends("MA", 0, lo, hi)
+            if c == 1:
+                terms = [(A("Bb"), y0), (A("Bbn"), m0)]
+            else:
+                terms = [(A("Bh"), y0), (A("Bhn"), m0), (A("Bh"), ends("YA", 1, lo, hi)), (A("Bhn"), ends("MA", 1, lo, hi)),
+                         (A("Bh"), H("hx"))]
+            terms += [(A("B8", rows=8), H("slb", (t * 3 + c - 1) * 128, 8)), (A("Bb"), H("c32"))]
+            mm(H("pD"), terms, True, False)
+        elif kind == "D":
+            mm(H("pD"), [(A("Bbn"), ends("YA", c, lo, hi)), (A("Bb"), ends("MA", c, lo, hi))], False, True)
+        elif kind == "H":
+            act(A("sg"), A("pD", 0, 128), f=fn.Sign)
+            mm(A("pX", 128, 256), [(A("Ip"), ends("YA", 1)), (A("In"), ends("MA", 1)), (A("In"), ends("YA", 0)), (A("Ip"), ends("MA", 0))])
+        elif kind == "h":
+            tt(A("hx"), A("pX", 128, 256), A("sg"), op.mult)
         elif kind == "S":
-            for n in range(9 if t == 0 else 0):
-                for d in (0, 8):
-                    scp(A("a8", n * 16 + d, n * 16 + d + 8), A("pK", n * 8, n * 8 + 8))
+            for d in range(2 if t == 0 else 0):
+                act(A("a8", d, 144, 2), A("pX", 0, 72))
         elif kind == "K":
             if t > 0:
-                cp(A("nW", 0, 128), A("L", i * 128, i * 128 + 128))
-                run("v", lambda: g.vector.tensor_reduce(T.cf[:, 32:33], T.pK[:, 80:88], AxisListType.X, op.add),
-                    [A("cf", 32, 33)], [A("pK", 80, 88)])
-                ts(A("ci", 32, 33), A("cf", 32, 33), -1.0, None, op.mult)
-                ts(A("ci", 33, 34), A("ci", 32, 33), 31, None, op.bitwise_and)
-                ts(A("kf", 2, 3), A("ci", 33, 34), 64.0, A("kf", 0, 1), op.mult, op.add)
-                ts(A("kf", 3, 4), A("kf", 2, 3), 64.0 * 77, None, op.add)
+                cp(A("kq", 0, 1), A("pX", 256, 257))
+                ts(A("kq", 1, 2), A("kq", 0, 1), 31, None, op.bitwise_and)
+                ts(A("kf", 0, 1), A("kq", 1, 2), 64.0, A("kf", 4, 5), op.mult, op.add)
+                ts(A("kf", 1, 3), A("kf", 5, 7), A("kf", 0, 1), None, op.add)
         elif kind == "P":
-            s = A("nW", c * 128, c * 128 + 128)
             if c == 0:
-                ts(A("pV", 128, 256), s, 64.0, A("kf", 2, 3), op.mult, op.add)
-            else:
-                ts(A("pV", 128, 256), s, 64.0, 64.0 * 77, op.mult, op.add)
-            cp(A("pV", 0, 128), s)
+                ts(A("NW", 0, 128), A("L", i * 128, i * 128 + 128), 64.0, None, op.mult)
+            cp(H("pV"), H("L", i * 128))
         elif kind == "C":
-            cp(A("Ui"), A("pU", 0, 128))
-            ts(A("ua"), A("Ui"), 4095, None, op.bitwise_and)
-            tt(A("P"), A("ua"), A("pV", 0, 128), op.mult)
-            p3 = A("P")
-            if c > 0:
-                ts(A("pV", 256, 384), A("P"), A("kf", 1 + c, 2 + c), None, op.add)
-                tt(A("h"), A("pE", 0, 128), A("thr"), op.is_le)
-                p3 = A("P3")
-                tt(p3, A("pV", 256, 384), A("h"), op.mult)
-            tt(A("Qi"), p3, A("pV", 128, 256), op.add)
-            ts(A("nW", (c + 1) * 128, (c + 2) * 128), A("Qi"), 6, 4095, op.arith_shift_right, op.bitwise_and)
-            cp(A("L", (i + 1) * 128, (i + 2) * 128), A("nW", (c + 1) * 128, (c + 2) * 128))
-            send_list(t, c + 1)
-        elif kind in ("X", "x", "y"):
-            px = px3 if c == 3 else A("pX", 8 * c, 8 * c + 8)
-            pu = pu3 if c == 3 else A("pX", 32 + 8 * c, 40 + 8 * c)
-            ys = [A("Y", c * 2048 + 16 * k + 15, c * 2048 + 2048, 256) for k in range(16)]
-            ms = [A("Mn", c * 2048 + 16 * k + 15, c * 2048 + 2048, 256) for k in range(16)]
-            if kind != "y":
-                mm(pu, [(blk("Wk", k), ys[k]) for k in range(16)])
-                mm(px, [(blk("Bk", k), ys[k]) for k in range(16)], True, False)
-            if kind != "x":
-                mm(px, [(blk("Bnk", k), ms[k]) for k in range(16)], False, True)
+            cp(H("Ui"), H("pU"))
+            ts(H("ua"), H("Ui"), 4095, None, op.bitwise_and)
+            tt(H("P"), H("ua"), H("pV"), op.mult)
+            if c == 0:
+                ts(H("pV", 128), H("P"), A("kf", 0, 1), None, op.add)
+            else:
+                tt(H("X"), H("P"), H("pD"), op.min)
+                ts(H("pV", 128), H("X"), A("kf", c, c + 1), 64.0 * 77 - 2097152.0, op.add, op.max)
+            tt(H("Qi"), H("pV", 128), H("NW", c * 128), op.add)
+            ts(H("NW", (c + 1) * 128), H("Qi"), 4095 * 64, None, op.bitwise_and)
+            ts(H("L", (i + 1) * 128), H("NW", (c + 1) * 128), 1.0 / 64, None, op.mult)
+            send_list(t, c + 1, h)
+        elif kind == "X":
+            mm(A("pC", 0, 24), [(pick("Zp", k), col("YA", k, 0, 3)) for k in range(16)]
+               + [(pick("Zn", k), col("MA", k, 0, 3)) for k in range(16)])
+        elif kind == "x":
+            mm(A("pZ", 8, 40), [(pick("Zw", k), col("YA", k, 0, 4)) for k in range(16)])
+            mm(A("pZ", 0, 8), [(pick("Zp", k), col("YA", k, 3, 4)) for k in range(16)], True, False)
+        elif kind == "y":
+            mm(A("pZ", 0, 8), [(pick("Zn", k), col("MA", k, 3, 4)) for k in range(16)], False, True)
         elif kind == "F":
-            mm(A("pY", 8 * c, 8 * c + 8), [(blk("Bk", k), A("YS", 16 * k + 15, 2048, 256)) for k in range(16)], True, False)
-        elif kind == "B":
-            mm(A("pY", 8 * c, 8 * c + 8), [(blk("Bnk", k), A("MS", 16 * k + 15, 2048, 256)) for k in range(16)], False, True)
-        elif kind in ("R", "r"):
-            (cp if kind == "R" else scp)(A("Er", i * 8, i * 8 + 8), A("pY", 8 * c, 8 * c + 8))
-            send_reply(t, c)
-        elif kind == "J" and c < 2:
-            for n in ([0, 1] if c == 0 else [2]):
-                cp(A("cat", 16 * n, 16 * n + 8), A("pX", 8 * n, 8 * n + 8))
-                tt(A("cat", 16 * n + 8, 16 * n + 16), A("pX", 8 * n, 8 * n + 8), A("Eq", (t * NL + n) * 8, (t * NL + n) * 8 + 8), op.add)
-            st = A("cat", 0, 16) if c == 0 else A("cat", 48, 64)
-            tt(A("dl", 0, 16), A("cat", 16 * c + 16, 16 * c + 32), st, op.subtract)
-            j = t * 3 + c
-            tt(A("HD", 16 * c, 16 * c + 16), A("dl", 0, 16), A("a8", j * 16, j * 16 + 16), op.is_le)
-            for d in (0, 8):
-                tt(A("dl", 16 + d, 24 + d), A("dl", d, d + 8), A("HD", 16 * c, 16 * c + 8), op.mult)
-            tt(A("cat", 48 + 16 * c, 64 + 16 * c), st, A("dl", 16, 32), op.add)
-            tt(A("rt", 8 * c, 8 * c + 8), A("HD", 16 * c, 16 * c + 8), A("HD", 16 * c + 8, 16 * c + 16), op.is_equal)
-        elif kind == "J" and c == 2:
-            cp(A("Ki", 0, 24), A("pX", 32, 56))
-            ts(A("Ki", 32, 56), A("Ki", 0, 24), 31, None, op.bitwise_and)
-            tt(A("K", 0, 24), A("Ki", 32, 56), A("cK", 0, 24), op.add)
-            j = t * 3 + 2
-            tt(A("cat", 80, 96), A("cat", 64, 80), A("a8", j * 16, j * 16 + 16), op.add)
-            tt(A("rt", 16, 24), A("rt", 0, 8), A("rt", 8, 16), op.mult)
-            tt(A("rt", 24, 32), A("rt", 0, 8), A("HD", 24, 32), op.mult)
-            tt(A("cf", 0, 8), A("HD", 8, 16), A("K", 8, 16), op.mult)
-            tt(A("cf", 8, 16), A("rt", 24, 32), A("K", 16, 24), op.mult)
-            tt(A("cf", 16, 24), A("K", 0, 8), A("cf", 0, 8), op.max)
-            tt(A("cf", 24, 32), A("cf", 16, 24), A("cf", 8, 16), op.max)
+            mm(A("pY", 0, 24), [(pick("Zp", k), col("YS", k, 0, 3)) for k in range(16)]
+               + [(pick("Zn", k), col("MS", k, 0, 3)) for k in range(16)])
+        elif kind == "R":
+            cp(A("Er", t * 32, t * 32 + 24), A("pY", 0, 24))
+            send_reply(t, 0, 24, "e%d" % (2 * t))
+        elif kind == "W":
+            mm(A("pW", 0, 128), [(A("Bp"), ends("YS", 3))], True, False)
+        elif kind == "w":
+            mm(A("pW", 0, 128), [(A("Bn"), ends("MS", 3))], False, True)
+        elif kind == "r":
+            scan(A("dg"), A("pW", 0, 128), A("dm"), op.max, op.add)
+            ts(A("Er", t * 32 + 24, t * 32 + 32), A("dg", 15, 128, 16), DG, None, op.add)
+            send_reply(t, 24, 32, "e%d" % (2 * t + 1))
         elif kind == "J":
-            cp(A("Ki", 24, 32), pu3)
-            tt(A("rt", 32, 40), A("cat", 88, 96), px3, op.subtract)
-            ts(A("Ki", 56, 64), A("Ki", 24, 32), 31, None, op.bitwise_and)
-            tt(A("rt", 40, 48), px3, A("cat", 80, 88), op.is_le)
-            tt(A("K", 24, 32), A("Ki", 56, 64), A("cK", 24, 32), op.add)
-            tt(A("rt", 48, 56), A("rt", 16, 24), A("K", 24, 32), op.mult)
+            cp(A("cat", 0, 48, 2), A("pC", 0, 24))
+            tt(A("cat", 1, 48, 2), A("pC", 0, 24), A("Eq", t * 32, t * 32 + 24), op.add)
+            st = A("cat", 0, 16)
+            for j in range(2):
+                a = (t * 3 + j) * 16
+                d, m, nx = [A("dl", 48 * j + 16 * n, 48 * j + 16 * n + 16) for n in range(3)]
+                tt(d, A("cat", 16 * j + 16, 16 * j + 32), st, op.subtract)
+                tt(A("HD", 16 * j, 16 * j + 16), d, A("a8", a, a + 16), op.is_le)
+                tt(m, d, A("HD", 16 * j, 16 * j + 16), op.mult)
+                tt(nx, st, m, op.add)
+                st = nx
+            a = (t * 3 + 2) * 16
+            tt(A("rt", 0, 16), A("HD", 0, 32, 2), A("HD", 1, 32, 2), op.is_equal)
+            tt(A("dl", 96, 112), st, A("a8", a, a + 16), op.add)
+            tt(A("HD", 33, 48, 2), A("rt", 0, 8), A("rt", 8, 16), op.mult)
+            tt(A("HD", 17, 32, 2), A("HD", 17, 32, 2), A("rt", 0, 8), op.mult)
+        elif kind == "Jk":
+            cp(A("Ki", 0, 32), A("pZ", 8, 40))
+            tt(A("rt", 16, 24), A("dl", 97, 112, 2), A("pZ", 0, 8), op.subtract)
+            ts(A("Ki", 32, 64), A("Ki", 0, 32), 31, None, op.bitwise_and)
+            tt(A("rt", 24, 32), A("pZ", 0, 8), A("dl", 96, 112, 2), op.is_le)
+            tt(A("K"), A("Ki", 32, 64), A("cK"), op.add)
+            tt(A("cf", 0, 24), A("HD", 1, 48, 2), A("K", 8, 32), op.mult)
+            tt(A("cf", 24, 32), A("K", 0, 8), A("cf", 0, 8), op.max)
+            tt(A("cf", 32, 40), A("cf", 24, 32), A("cf", 8, 16), op.max)
         elif kind == "Z":
             last = t == RO - 1
-            n = (t * NL + 3) * 8
-            tt(A("HD", 32, 40), A("Eq", n, n + 8), A("rt", 32, 40), op.is_le)
-            tt(A("HD", 40, 48), A("HD", 32, 40), A("rt", 48, 56), op.mult)
-            tt(A("ci", 0, 8), A("HD", 40, 48), A("cf", 24, 32), op.max)
+            n = t * 32 + 24
+            tt(A("rt", 32, 40), A("Eq", n, n + 8), A("rt", 16, 24), op.is_le)
+            tt(A("rt", 40, 48), A("rt", 32, 40), A("cf", 16, 24), op.mult)
+            tt(A("ci", 0, 8), A("rt", 40, 48), A("cf", 32, 40), op.max)
             ts(A("ci", 8, 16), A("ci", 0, 8), 5, None, op.arith_shift_right)
-            ts(A("ci", 16, 24), A("ci", 0, 8), 4095, None, op.bitwise_and)
             if last:
-                cp(A("o3", 0, 4), A("ci", 16, 20))
-                ts(A("o3", 4, 8), A("ci", 20, 24), -2048.0, None, op.add)
-                sgather(A("old", 0, 64), A("tab", 0, 2048), A("o3", 0, 4))
-                sgather(A("old", 64, 128), A("tab", 2048, 4096), A("o3", 4, 8))
-                ts(A("o2"), A("ci", 8, 16), 16.0, 15.0, op.mult, op.add)
+                ts(A("ci", 16, 24), A("ci", 0, 8), 2047, None, op.bitwise_and)
             else:
-                cp(A("o1"), A("ci", 8, 16))
-                cp(A("o3"), A("ci", 16, 24))
-                sgather(A("old"), A("tab"), A("o3"))
-                vgather(A("L", (i_next(t)) * 128, (i_next(t)) * 128 + 128), A("nW"), A("o1"))
-                send_list(t + 1, 0)
-                ts(A("o2"), A("ci", 8, 16), 16.0, 15.0, op.mult, op.add)
+                ts(A("ci", 16, 24), A("ci", 0, 8), 4095, None, op.bitwise_and)
+            cp(A("o13"), A("ci", 8, 24))
+            o1 = W("o13", 0, 8)
             parts = [(0, 64), (64, 128)] if last else [(0, 128)]
             for a, b in parts:
-                yw, of = A("Y"), A("o2", a // 16, b // 16)
+                sgather(W("old", a, b), W("tab", 32 * a, 32 * b), W("o13", 8 + a // 16, 8 + b // 16))
+            if not last:
+                nxt = (t + 1) * NL * 128
+                ts(W("L", nxt, nxt + 128), W("NW"), 1.0 / 64, None, op.mult, off=o1)
+                send_list(t + 1, 0)
+            ts(A("o2"), o1, 16.0, 15.0, op.mult, op.add)
+            for a, b in parts:
+                yw, of = W("YA"), W("o2", a // 16, b // 16)
                 run("v", lambda: g.vector.tensor_tensor(T.sm[:, a:b], yw[0].indirect(of[0]), T.old[:, a:b], op.add),
-                    [A("sm", a, b)], [yw, of, A("old", a, b)])
+                    [W("sm", a, b)], [yw, of, W("old", a, b)])
                 ts(A("sn", a, b), A("sm", a, b), 1, None, op.arith_shift_right)
-                win, of3 = A("tab", 32 * a, 32 * b), A("o3", a // 16, b // 16)
-                run("v", lambda: g.vector.tensor_copy(win[0].indirect(of3[0]), T.sn[:, a:b]), [win], [A("sn", a, b), of3])
+                win, of3 = W("tab", 32 * a, 32 * b), W("o13", 8 + a // 16, 8 + b // 16)
+                run("v", lambda: g.vector.tensor_copy(win[0].indirect(of3[0]), T.sn[:, a:b]), [win], [W("sn", a, b), of3])
                 if last:
                     dma("y" if a == 0 else "s", ext(T.yx[:, 32 * a:32 * b]), win, "st0" if a == 0 else "st1")
             if last:
-                cp(A("o1"), A("ci", 8, 16))
-                vgather(A("fin"), A("nW"), A("o1"))
-                dma("y", ext(T.yc[:, :]), A("fin"), "st2")
+                ts(W("fin"), W("NW"), 1.0 / 64, None, op.mult, off=o1)
+                dma("y", ext(T.yc[:, :]), W("fin"), "st2")
             else:
-                tt(A("rt", 56, 64), A("HD", 32, 40), A("rt", 40, 48), op.is_equal)
-                tt(A("r3"), A("rt", 56, 64), A("rt", 16, 24), op.mult)
-                mm(A("pK", 80, 88), [(A("ones"), A("r3"))])
-
-    def i_next(t):
-        return (t + 1) * NL
+                tt(A("rt", 48, 56), A("rt", 32, 40), A("rt", 24, 32), op.is_equal)
+                tt(A("r3"), A("rt", 48, 56), A("HD", 33, 48, 2), op.mult)
+                mm(A("pX", 256, 257), [(A("neg"), A("r3", n, n + 1)) for n in range(8)])
 
     for t in range(RO):
         for w in ORDER.split():

@@ -2,17 +2,15 @@ from concourse.mybir import AluOpType, ActivationFunctionType
 
 RO, NL = 3, 4
 BIG = 2.0 ** 25
-DG = 8192.0
+DG = 2.0 ** 18
 SCRATCH = {
     "tab": ("sbuf", [128, 4096], "bfloat16"),
     "chI": ("sbuf", [128, 128], "int32"),
     "NW": ("sbuf", [128, 512], "int32"),
     "L": ("sbuf", [128, RO * NL * 128], "uint16"),
     "Lr": ("sbuf", [128, RO * NL * 128], "uint16"),
-    "gA0": ("sbuf", [128, 2048], "bfloat16"),
-    "gA1": ("sbuf", [128, 2048], "bfloat16"),
-    "gS0": ("sbuf", [128, 2048], "bfloat16"),
-    "gS1": ("sbuf", [128, 2048], "bfloat16"),
+    "gA": ("sbuf", [128, 8192], "bfloat16"),
+    "gS": ("sbuf", [128, 8192], "bfloat16"),
     "YA": ("sbuf", [128, 8192], "bfloat16"),
     "MA": ("sbuf", [128, 8192], "bfloat16"),
     "YS": ("sbuf", [128, 8192], "bfloat16"),
@@ -24,7 +22,8 @@ SCRATCH = {
     "rowb": ("sbuf", [128, 128], "float32"),
     "rowj": ("sbuf", [128, 144], "float32"),
     "rowx": ("sbuf", [128, 128], "float32"),
-    "dm": ("sbuf", [128, 128], "float32"),
+    "dm": ("sbuf", [128, 256], "float32"),
+    "dz": ("sbuf", [128, 256], "float32"),
     "dt": ("sbuf", [128, 256], "float32"),
     "dg": ("sbuf", [128, 128], "float32"),
     "Bp": ("sbuf", [128, 128], "bfloat16"),
@@ -92,10 +91,12 @@ SEMAPHORES = (["qv", "qs", "qp", "qg", "sent", "ld0", "ld1", "ld2", "ld3", "st0"
               + ["l%d%s" % (i, h) for i in range(RO * NL) for h in ("", "a", "b")]
               + ["e%d%s" % (i, h) for i in range(RO * 2) for h in ("", "a", "b")])
 
-ORDER = ("GA0a vGA0b K P0 YA0 U0 C0 GS0a GS0b GA1a GA1b MA0 e1 P1 YS0a MS0a YS0b MS0b "
-         "YA1a MA1a GS1a GS1b YA1b U1 MA1b D1 C1 H GA2a GA2b YS1a MS1a h e2 P2 YS1b MS1b "
-         "YA2a MA2a GS2a GS2b YA2b U2 MA2b D2 C2 GA3a GA3b X S YS2 MS2 F GS3a GS3b YA3a MA3a R YA3b x MA3b y "
-         "YS3a MS3a YS3b W MS3b w r J Jk Z")
+PARTS = {"": (0, 128), "a": (0, 64), "b": (64, 128), "c": (0, 32), "d": (32, 64), "e": (64, 96), "f": (96, 128),
+         "g": (0, 96), "h": (32, 128)}
+ORDER = ("GA0a k vGA0b YA0 U0 K+P0 C0a+C0b L1 GS0 GA1a GA1b MA0 e1 vQ P1 YS0 MS0 "
+         "YA1a MA1a GS1 YA1b U1 MA1b D1 C1a+C1b L2 H GA2a GA2b YS1 h e2 MS1 P2 "
+         "YA2a MA2a GS2 YA2b U2 MA2b D2 C2a+C2b L3 GA3a GA3b X XX S j YS2 F MS2 FF GS3a GS3b YA3a vR MA3a YA3b x MA3b y "
+         "YS3a MS3a YS3b W MS3b w r J+Ja Jb Z")
 
 
 def rank_program(g, core, T, topo):
@@ -146,20 +147,37 @@ def rank_program(g, core, T, topo):
             log[i[1]] = [a for a in log[i[1]] if a[2] or a[3] != q or not (i[2] <= a[0] and a[1] <= i[3])]
             log[i[1]].append((i[2], i[3], False, q, s, v, clock))
 
+    jobs = []
+
     def run(q, call, outs, ins):
-        need(q, outs, ins)
-        cnt[q] += 1
-        call().then_inc(T.sem["q" + q], 1)
-        clock = dict(known[q])
-        clock["q" + q] = cnt[q]
-        note(q, outs, ins, "q" + q, cnt[q], clock)
+        def job():
+            need(q, outs, ins)
+            cnt[q] += 1
+            call().then_inc(T.sem["q" + q], 1)
+            clock = dict(known[q])
+            clock["q" + q] = cnt[q]
+            note(q, outs, ins, "q" + q, cnt[q], clock)
+        jobs.append(job)
 
     def dma(q, out, in_, s):
-        o = [out] if out[1] else []
-        i = [in_] if in_[1] else []
-        need(q, o, i)
-        Q[q].dma_start(out[0], in_[0]).then_inc(T.sem[s], 16)
-        note("dma", o, i, s, 16, dict(known[q]))
+        def job():
+            o = [out] if out[1] else []
+            i = [in_] if in_[1] else []
+            need(q, o, i)
+            Q[q].dma_start(out[0], in_[0]).then_inc(T.sem[s], 16)
+            note("dma", o, i, s, 16, dict(known[q]))
+        jobs.append(job)
+
+    def issue(*lists):
+        for n in range(max(len(x) for x in lists)):
+            for x in lists:
+                if n < len(x):
+                    x[n]()
+
+    def taken():
+        x = list(jobs)
+        del jobs[:]
+        return x
 
     def ext(ap):
         return (ap, None, 0, 0)
@@ -204,13 +222,21 @@ def rank_program(g, core, T, topo):
         run("s", lambda: g.scalar.activation(out[0], win[0].indirect(off[0]), fn.Copy), [out], [win, off])
 
     def act(out, in_, scale=1.0, bias=0.0, f=None):
-        ins = [in_] + ([scale] if isinstance(scale, tuple) else [])
-        run("s", lambda: g.scalar.activation(out[0], in_[0], f or fn.Copy, bias=bias, scale=val(scale)), [out], ins)
+        ins = [in_] + [x for x in (scale, bias) if isinstance(x, tuple)]
+        run("s", lambda: g.scalar.activation(out[0], in_[0], f or fn.Copy, bias=val(bias), scale=val(scale)), [out], ins)
+
+    def gadd(out, win, off, b):
+        run("v", lambda: g.vector.tensor_tensor(out[0], win[0].indirect(off[0]), b[0], op.add), [out], [win, off, b])
+
+    def scatter(win, off, in_):
+        run("v", lambda: g.vector.tensor_copy(win[0].indirect(off[0]), in_[0]), [win], [in_, off])
+
+    def mm1(out, l, r, st, sp):
+        run("p", lambda: g.tensor.matmul(out[0], l[0], r[0], st, sp), [out], [l, r])
 
     def mm(out, pairs, first=True, last=True):
         for n, (l, r) in enumerate(pairs):
-            st, sp = first and n == 0, last and n == len(pairs) - 1
-            run("p", lambda: g.tensor.matmul(out[0], l[0], r[0], st, sp), [out], [l, r])
+            mm1(out, l, r, first and n == 0, last and n == len(pairs) - 1)
 
     def iota(out, pattern, base, cm):
         kw = {} if SCRATCH[out[1]][2] == "int32" else {"allow_small_or_imprecise_dtypes": True}
@@ -220,15 +246,17 @@ def rank_program(g, core, T, topo):
     sends = [0]
 
     def send(dst, out, in_, s):
-        need("g", [], [in_])
-        rid, pid, _ = topo.addr(dst)
-        m = sum(1 << e for e in topo.engines(core, dst)[:n_eng])
-        g.remote_dma(out[0], in_[0], T.sem[s], T.sem.sent, pid, rid, m)
-        sends[0] += n_eng
-        note("x", [out], [], s, n_eng, {})
+        def job():
+            need("g", [], [in_])
+            rid, pid, _ = topo.addr(dst)
+            m = sum(1 << e for e in topo.engines(core, dst)[:n_eng])
+            g.remote_dma(out[0], in_[0], T.sem[s], T.sem.sent, pid, rid, m)
+            sends[0] += n_eng
+            note("x", [out], [], s, n_eng, {})
+        jobs.append(job)
 
     def half(x):
-        return {"": (0, 128), "a": (0, 64), "b": (64, 128)}[x]
+        return PARTS[x]
 
     def send_list(t, c, h=""):
         i = t * NL + c
@@ -241,50 +269,50 @@ def rank_program(g, core, T, topo):
         send(p, W("Eq", t * 32 + lo, t * 32 + hi), W("Er", t * 32 + lo, t * 32 + hi), s)
 
     dma("y", W("chI"), ext(T.ch[:, :]), "ld0")
-    dma("s", W("wI"), ext(T.wt[:, :]), "ld1")
-    dma("y", W("tab"), ext(T.xt[:, :]), "ld2")
-    dma("s", A("slI", rows=8), ext(T.sl[:, :]), "ld3")
+    dma("s", W("tab"), ext(T.xt[:, :]), "ld2")
+    dma("y", A("slI", rows=8), ext(T.sl[:, :]), "ld3")
+    dma("y", W("wI"), ext(T.wt[:, :]), "ld1")
     iota(A("kI", 0, 1), [[0, 1]], 0, 1)
+    iota(A("pf", 3, 4), [[0, 1]], 0, 16)
     iota(A("rowb"), [[16, 8], [0, 16]], 0, 0)
     iota(A("rowj"), [[1, 144]], -15, 0)
     iota(A("rowx"), [[0, 8], [1, 16]], 0, 0)
     iota(A("cKi"), [[4096, 4], [512, 8]], 0, 0)
-    fill(A("mx"), 1.0)
-    fill(A("mx", 0, 2048, 16), 0.0)
-    act(A("mn"), A("mx"), -512.0, 512.0)
+    iota(A("kf", 4, 7), [[64 * 77, 3]], 0, 0)
+    fill(A("mx", 0, 1024), 1.0)
+    fill(A("neg"), -1.0)
+    fill(A("mx", 0, 1024, 16), 0.0)
     ts(A("kI", 1, 2), A("kI", 0, 1), 112, None, op.bitwise_and)
     ts(A("kI", 2, 3), A("kI", 0, 1), 15, None, op.bitwise_and)
-    fill(A("neg"), -1.0)
-    cp(A("pf", 0, 3), A("kI", 0, 3))
-    ts(A("pf", 3, 4), A("kI", 0, 1), 16.0, None, op.mult)
     fill(A("c32"), 1.0 / 32)
-    cp(A("L", 0, 128), A("chI"))
-    send_list(0, 0)
+    act(A("mx", 1024, 2048), A("mx", 0, 1024))
+    act(A("mn"), A("mx"), -512.0, 512.0)
+    cp(A("pf", 0, 3), A("kI", 0, 3))
     p_, blk_, k_, p16_ = [A("pf", n, n + 1) for n in range(4)]
+    ts(A("B8"), A("rowb"), p16_, BIG, op.is_equal, op.mult)
     ts(A("Bp"), A("rowb"), blk_, None, op.is_equal)
+    ts(A("kf", 7, 8), k_, 64.0 * 613, -1048576.0, op.mult, op.add)
     ts(A("Zp"), A("rowj"), blk_, None, op.is_equal)
     ts(A("Ip"), A("rowj", 15, 143), p_, None, op.is_equal)
     ts(A("Z8"), A("rowj"), p16_, None, op.is_equal)
-    ts(A("B8"), A("rowb"), p16_, BIG, op.is_equal, op.mult)
-    for n, m in ((0, 4032), (1, 63), (2, 31)):
-        ts(A("wq", n, n + 1), A("wI"), m, None, op.bitwise_and)
-    ts(A("kf", 4, 5), k_, 64.0 * 613, -1048576.0, op.mult, op.add)
-    cp(A("wf", 0, 3), A("wq", 0, 3))
-    for j in range(3):
-        ts(A("kf", j, j + 1), A("kf", 4, 5), 64.0 * 77 * j, None, op.add)
-    for j in (1, 2):
-        fill(A("kf", 4 + j, 5 + j), 64.0 * 77 * j)
-    for name, src, x in (("Wh", "Bp", A("wf", 0, 1)), ("Wl", "Bp", A("wf", 1, 2)), ("Bb", "Bp", BIG), ("Bbn", "Bp", -BIG),
-                         ("Bn", "Bp", -1.0), ("Bh", "Bp", BIG / 2), ("Bhn", "Bp", -BIG / 2), ("In", "Ip", -1.0),
-                         ("Zn", "Zp", -1.0), ("Zw", "Zp", A("wf", 2, 3))):
-        act(A(name), A(src), x)
+    ts(A("wf", 3, 4), k_, 32.0, None, op.mult)
     ts(A("dt", 0, 128), A("rowx"), k_, -DG, op.is_lt, op.mult)
     ts(A("dt", 128, 256), A("rowx"), k_, DG, op.is_equal, op.mult)
-    ts(A("wf", 3, 4), k_, 32.0, None, op.mult)
-    tt(A("dm"), A("dt", 0, 128), A("dt", 128, 256), op.add)
+    cp(A("L", 0, 128), A("chI"))
+    send_list(0, 0)
+    tt(A("dm", 0, 128), A("dt", 0, 128), A("dt", 128, 256), op.add)
     ts(A("cK"), A("cKi"), A("wf", 3, 4), None, op.add)
+    ts(A("kf", 0, 3), A("kf", 4, 7), A("kf", 7, 8), None, op.add)
     ts(A("dm", 15, 128, 16), A("dm", 15, 128, 16), -2 * DG, None, op.add)
     cp(A("slb", rows=8), A("slI", rows=8))
+    for n, m in ((0, 4064), (1, 31)):
+        ts(A("wq", n, n + 1), A("wI"), m, None, op.bitwise_and)
+    cp(A("wf", 0, 2), A("wq", 0, 2))
+    for name, src, x in (("Bb", "Bp", BIG), ("Bbn", "Bp", -BIG), ("Bn", "Bp", -1.0), ("Bh", "Bp", BIG / 2),
+                         ("Bhn", "Bp", -BIG / 2), ("In", "Ip", -1.0), ("Zn", "Zp", -1.0),
+                         ("Wh", "Bp", A("wf", 0, 1)), ("Wl", "Bp", A("wf", 1, 2)), ("Zw", "Zp", A("wf", 1, 2))):
+        act(A(name), A(src), x)
+    act(A("dm", 128, 256), A("dm", 0, 128))
 
     def pick(name, k, rows=128):
         return A(name, 15 - k, 143 - k, rows=rows)
@@ -300,22 +328,22 @@ def rank_program(g, core, T, topo):
     def piece(t, w):
         onv = w[0] == "v"
         w = w[1:] if onv else w
-        kind = w.rstrip("0123ab")
-        rest = w[len(kind):]
-        c = int(rest[0]) if rest else 0
-        h = rest[1:]
+        n = min([w.find(x) for x in "0123" if x in w] + [len(w)])
+        kind, c, h = w[:n], int(w[n:n + 1] or 0), w[n + 1:]
         lo, hi = half(h)
         i = t * NL + c
 
         def H(name, base=0, rows=128):
             return A(name, base + lo, base + hi, rows=rows)
 
-        if kind in ("GA", "GS"):
+        if kind == "_":
+            jobs.append(lambda: None)
+        elif kind in ("GA", "GS"):
             own = kind == "GA"
-            out = W(("gA%d" if own else "gS%d") % (c % 2), lo * 16, hi * 16)
+            out = W("gA" if own else "gS", c * 2048 + lo * 16, c * 2048 + hi * 16)
             (vgather if onv else sgather)(out, W("tab"), W("L" if own else "Lr", i * 128 + lo, i * 128 + hi))
         elif kind in ("YA", "YS", "MA", "MS"):
-            out, src = A(kind, c * 2048 + lo * 16, c * 2048 + hi * 16), A("g%s%d" % (kind[1], c % 2), lo * 16, hi * 16)
+            out, src = [A(n, c * 2048 + lo * 16, c * 2048 + hi * 16) for n in (kind, "g" + kind[1])]
             if kind[0] == "Y":
                 scan(out, A("mx", lo * 16, hi * 16), src, op.mult, op.max)
             else:
@@ -341,53 +369,99 @@ def rank_program(g, core, T, topo):
         elif kind == "S":
             for d in range(2 if t == 0 else 0):
                 act(A("a8", d, 144, 2), A("pX", 0, 72))
+            for j in range(RO if t == 0 and "Jw" in ORDER else 0):
+                act(A("a8", 48 * j + 32, 48 * j + 48), A("a8", 48 * j + 32, 48 * j + 48), bias=-DG)
+        elif kind == "k":
+            if t > 0:
+                tt(A("rt", 48, 56), A("rt", 32, 40), A("rt", 24, 32), op.is_equal)
+                tt(A("r3"), A("rt", 48, 56), A("HD", 33, 48, 2), op.mult)
+                mm(A("pX", 256, 257), [(A("neg"), A("r3", n, n + 1)) for n in range(8)])
         elif kind == "K":
             if t > 0:
                 cp(A("kq", 0, 1), A("pX", 256, 257))
                 ts(A("kq", 1, 2), A("kq", 0, 1), 31, None, op.bitwise_and)
-                ts(A("kf", 0, 1), A("kq", 1, 2), 64.0, A("kf", 4, 5), op.mult, op.add)
-                ts(A("kf", 1, 3), A("kf", 5, 7), A("kf", 0, 1), None, op.add)
+                ts(A("kf", 0, 1), A("kq", 1, 2), 64.0, A("kf", 7, 8), op.mult, op.add)
+        elif kind == "Q":
+            if t > 0:
+                if onv:
+                    ts(A("kf", 1, 3), A("kf", 5, 7), A("kf", 0, 1), None, op.add)
+                else:
+                    act(A("kf", 1, 3), A("kf", 5, 7), bias=A("kf", 0, 1), f=fn.Identity)
         elif kind == "P":
             if c == 0:
                 ts(A("NW", 0, 128), A("L", i * 128, i * 128 + 128), 64.0, None, op.mult)
-            cp(H("pV"), H("L", i * 128))
+            else:
+                cp(H("pV"), H("L", i * 128))
         elif kind == "C":
             cp(H("Ui"), H("pU"))
             ts(H("ua"), H("Ui"), 4095, None, op.bitwise_and)
-            tt(H("P"), H("ua"), H("pV"), op.mult)
             if c == 0:
-                ts(H("pV", 128), H("P"), A("kf", 0, 1), None, op.add)
+                tt(H("P"), H("ua"), H("NW"), op.mult)
+                ts(H("pV", 128), H("P"), 1.0 / 64, A("kf", 0, 1), op.mult, op.add)
             else:
+                tt(H("P"), H("ua"), H("pV"), op.mult)
                 tt(H("X"), H("P"), H("pD"), op.min)
                 ts(H("pV", 128), H("X"), A("kf", c, c + 1), 64.0 * 77 - 2097152.0, op.add, op.max)
             tt(H("Qi"), H("pV", 128), H("NW", c * 128), op.add)
             ts(H("NW", (c + 1) * 128), H("Qi"), 4095 * 64, None, op.bitwise_and)
             ts(H("L", (i + 1) * 128), H("NW", (c + 1) * 128), 1.0 / 64, None, op.mult)
-            send_list(t, c + 1, h)
+        elif kind == "L":
+            send_list(t, c, h)
         elif kind == "X":
-            mm(A("pC", 0, 24), [(pick("Zp", k), col("YA", k, 0, 3)) for k in range(16)]
-               + [(pick("Zn", k), col("MA", k, 0, 3)) for k in range(16)])
+            mm(A("pC", 0, 24), [(pick("Zp", k), col("YA", k, 0, 3)) for k in range(16)], True, False)
+        elif kind == "XX":
+            mm(A("pC", 0, 24), [(pick("Zn", k), col("MA", k, 0, 3)) for k in range(16)], False, True)
         elif kind == "x":
             mm(A("pZ", 8, 40), [(pick("Zw", k), col("YA", k, 0, 4)) for k in range(16)])
             mm(A("pZ", 0, 8), [(pick("Zp", k), col("YA", k, 3, 4)) for k in range(16)], True, False)
         elif kind == "y":
             mm(A("pZ", 0, 8), [(pick("Zn", k), col("MA", k, 3, 4)) for k in range(16)], False, True)
+        elif kind == "u":
+            mm(A("pC", 24, 48), [(pick("Zw", k), col("YA", k, 0, 3)) for k in range(16)])
+        elif kind == "xw":
+            mm(A("pZ", 128, 256), [(A("Wl"), ends("YA", 3))])
+            mm(A("pZ", 0, 128), [(A("Bp"), ends("YA", 3))], True, False)
+        elif kind == "yw":
+            mm(A("pZ", 0, 128), [(A("Bn"), ends("MA", 3))], False, True)
+        elif kind == "Jw":
+            scan(A("dz"), A("pZ", 0, 256), A("dm"), op.max, op.add)
+            cp(A("Ki", 0, 24), A("pC", 24, 48))
+            ts(A("Ki", 24, 32), A("dz", 128 + 15, 256, 16), DG, None, op.add)
+            tt(A("rt", 16, 24), A("dl", 97, 112, 2), A("dz", 15, 128, 16), op.subtract)
+            ts(A("Ki", 32, 64), A("Ki", 0, 32), 31, None, op.bitwise_and)
+            tt(A("rt", 24, 32), A("dz", 15, 128, 16), A("dl", 96, 112, 2), op.is_le)
+            tt(A("K"), A("Ki", 32, 64), A("cK"), op.add)
+            tt(A("cf", 0, 24), A("HD", 1, 48, 2), A("K", 8, 32), op.mult)
+            tt(A("cf", 24, 32), A("K", 0, 8), A("cf", 0, 8), op.max)
+            tt(A("cf", 32, 40), A("cf", 24, 32), A("cf", 8, 16), op.max)
+        elif kind == "Ja":
+            cp(A("Ki", 0, 32), A("pZ", 8, 40))
+            ts(A("Ki", 32, 64), A("Ki", 0, 32), 31, None, op.bitwise_and)
+            tt(A("K"), A("Ki", 32, 64), A("cK"), op.add)
+        elif kind == "Jb":
+            tt(A("cf", 0, 24), A("HD", 1, 48, 2), A("K", 8, 32), op.mult)
+            tt(A("rt", 16, 24), A("dl", 97, 112, 2), A("pZ", 0, 8), op.subtract)
+            tt(A("cf", 24, 32), A("K", 0, 8), A("cf", 0, 8), op.max)
+            tt(A("rt", 24, 32), A("pZ", 0, 8), A("dl", 96, 112, 2), op.is_le)
+            tt(A("cf", 32, 40), A("cf", 24, 32), A("cf", 8, 16), op.max)
         elif kind == "F":
-            mm(A("pY", 0, 24), [(pick("Zp", k), col("YS", k, 0, 3)) for k in range(16)]
-               + [(pick("Zn", k), col("MS", k, 0, 3)) for k in range(16)])
+            mm(A("pY", 0, 24), [(pick("Zp", k), col("YS", k, 0, 3)) for k in range(16)], True, False)
+        elif kind == "FF":
+            mm(A("pY", 0, 24), [(pick("Zn", k), col("MS", k, 0, 3)) for k in range(16)], False, True)
         elif kind == "R":
-            cp(A("Er", t * 32, t * 32 + 24), A("pY", 0, 24))
+            (cp if onv else act)(A("Er", t * 32, t * 32 + 24), A("pY", 0, 24))
             send_reply(t, 0, 24, "e%d" % (2 * t))
         elif kind == "W":
-            mm(A("pW", 0, 128), [(A("Bp"), ends("YS", 3))], True, False)
+            mm(H("pW"), [(A("Bp"), ends("YS", 3, lo, hi))], True, False)
         elif kind == "w":
-            mm(A("pW", 0, 128), [(A("Bn"), ends("MS", 3))], False, True)
+            mm(H("pW"), [(A("Bn"), ends("MS", 3, lo, hi))], False, True)
         elif kind == "r":
-            scan(A("dg"), A("pW", 0, 128), A("dm"), op.max, op.add)
-            ts(A("Er", t * 32 + 24, t * 32 + 32), A("dg", 15, 128, 16), DG, None, op.add)
-            send_reply(t, 24, 32, "e%d" % (2 * t + 1))
+            scan(H("dg"), H("pW"), H("dm"), op.max, op.add)
+            ts(A("Er", t * 32 + 24 + lo // 16, t * 32 + 24 + hi // 16), A("dg", lo + 15, hi, 16), DG, None, op.add)
+            send_reply(t, 24 + lo // 16, 24 + hi // 16, "e%d%s" % (2 * t + 1, h))
+        elif kind == "j":
+            (cp if onv else act)(A("cat", 0, 48, 2), A("pC", 0, 24))
         elif kind == "J":
-            cp(A("cat", 0, 48, 2), A("pC", 0, 24))
             tt(A("cat", 1, 48, 2), A("pC", 0, 24), A("Eq", t * 32, t * 32 + 24), op.add)
             st = A("cat", 0, 16)
             for j in range(2):
@@ -434,25 +508,25 @@ def rank_program(g, core, T, topo):
                 send_list(t + 1, 0)
             ts(A("o2"), o1, 16.0, 15.0, op.mult, op.add)
             for a, b in parts:
-                yw, of = W("YA"), W("o2", a // 16, b // 16)
-                run("v", lambda: g.vector.tensor_tensor(T.sm[:, a:b], yw[0].indirect(of[0]), T.old[:, a:b], op.add),
-                    [W("sm", a, b)], [yw, of, W("old", a, b)])
+                gadd(W("sm", a, b), W("YA"), W("o2", a // 16, b // 16), W("old", a, b))
                 ts(A("sn", a, b), A("sm", a, b), 1, None, op.arith_shift_right)
-                win, of3 = W("tab", 32 * a, 32 * b), W("o13", 8 + a // 16, 8 + b // 16)
-                run("v", lambda: g.vector.tensor_copy(win[0].indirect(of3[0]), T.sn[:, a:b]), [win], [W("sn", a, b), of3])
+                win = W("tab", 32 * a, 32 * b)
+                scatter(win, W("o13", 8 + a // 16, 8 + b // 16), W("sn", a, b))
                 if last:
                     dma("y" if a == 0 else "s", ext(T.yx[:, 32 * a:32 * b]), win, "st0" if a == 0 else "st1")
             if last:
                 ts(W("fin"), W("NW"), 1.0 / 64, None, op.mult, off=o1)
                 dma("y", ext(T.yc[:, :]), W("fin"), "st2")
-            else:
-                tt(A("rt", 48, 56), A("rt", 32, 40), A("rt", 24, 32), op.is_equal)
-                tt(A("r3"), A("rt", 48, 56), A("HD", 33, 48, 2), op.mult)
-                mm(A("pX", 256, 257), [(A("neg"), A("r3", n, n + 1)) for n in range(8)])
 
+    issue(taken())
     for t in range(RO):
         for w in ORDER.split():
-            piece(t, w)
+            chains = []
+            for x in w.split("+"):
+                for y in x.split("."):
+                    piece(t, y)
+                chains.append(taken())
+            issue(*chains)
 
     for q in "vspg":
         g.wait_ge(T.sem["q" + q], cnt[q])

@@ -2,7 +2,7 @@ from concourse.mybir import AluOpType, ActivationFunctionType
 
 RO, NL = 3, 4
 BIG = 2.0 ** 25
-DG = 2.0 ** 18
+DG = BIG * 2.0 ** 13
 SCRATCH = {
     "tab": ("sbuf", [128, 4096], "bfloat16"),
     "chI": ("sbuf", [128, 128], "int32"),
@@ -15,44 +15,33 @@ SCRATCH = {
     "MA": ("sbuf", [128, 8192], "bfloat16"),
     "YS": ("sbuf", [128, 8192], "bfloat16"),
     "MS": ("sbuf", [128, 8192], "bfloat16"),
-    "Er": ("sbuf", [128, RO * 32], "float32"),
-    "Eq": ("sbuf", [128, RO * 32], "float32"),
+    "Er": ("sbuf", [128, RO * 48], "float32"),
+    "Eq": ("sbuf", [128, RO * 48], "float32"),
     "mx": ("sbuf", [128, 2048], "bfloat16"),
     "mn": ("sbuf", [128, 2048], "bfloat16"),
-    "rowb": ("sbuf", [128, 128], "float32"),
-    "rowj": ("sbuf", [128, 144], "float32"),
     "rowx": ("sbuf", [128, 128], "float32"),
-    "dm": ("sbuf", [128, 256], "float32"),
-    "dz": ("sbuf", [128, 256], "float32"),
-    "dt": ("sbuf", [128, 256], "float32"),
+    "dm": ("sbuf", [128, 128], "float32"),
     "dg": ("sbuf", [128, 128], "float32"),
-    "Bp": ("sbuf", [128, 128], "bfloat16"),
-    "Bn": ("sbuf", [128, 128], "bfloat16"),
-    "Bb": ("sbuf", [128, 128], "bfloat16"),
-    "Bbn": ("sbuf", [128, 128], "bfloat16"),
-    "Bh": ("sbuf", [128, 128], "bfloat16"),
-    "Bhn": ("sbuf", [128, 128], "bfloat16"),
+    "big": ("sbuf", [128, 256], "bfloat16"),
+    "one": ("sbuf", [128, 288], "bfloat16"),
+    "B2": ("sbuf", [128, 256], "bfloat16"),
     "B8": ("sbuf", [128, 128], "bfloat16"),
     "Wh": ("sbuf", [128, 128], "bfloat16"),
     "Wl": ("sbuf", [128, 128], "bfloat16"),
-    "Ip": ("sbuf", [128, 128], "bfloat16"),
-    "In": ("sbuf", [128, 128], "bfloat16"),
-    "neg": ("sbuf", [128, 128], "bfloat16"),
-    "c32": ("sbuf", [128, 128], "bfloat16"),
+    "I2": ("sbuf", [128, 288], "bfloat16"),
     "sg": ("sbuf", [128, 128], "bfloat16"),
     "hx": ("sbuf", [128, 128], "bfloat16"),
-    "Zp": ("sbuf", [128, 144], "bfloat16"),
-    "Zn": ("sbuf", [128, 144], "bfloat16"),
+    "Z2": ("sbuf", [128, 288], "bfloat16"),
     "Zw": ("sbuf", [128, 144], "bfloat16"),
-    "Z8": ("sbuf", [128, 144], "bfloat16"),
+    "Z8": ("sbuf", [128, 288], "bfloat16"),
     "slI": ("sbuf", [128, 1152], "int32"),
     "slb": ("sbuf", [128, 1152], "bfloat16"),
-    "a8": ("sbuf", [128, 144], "float32"),
+    "a8": ("sbuf", [128, RO * 32], "float32"),
     "wI": ("sbuf", [128, 1], "int32"),
     "wq": ("sbuf", [128, 4], "int32"),
     "wf": ("sbuf", [128, 4], "float32"),
     "kI": ("sbuf", [128, 4], "int32"),
-    "pf": ("sbuf", [128, 4], "float32"),
+    "pf": ("sbuf", [128, 8], "float32"),
     "kf": ("sbuf", [128, 8], "float32"),
     "kq": ("sbuf", [128, 2], "int32"),
     "cKi": ("sbuf", [128, 32], "float32"),
@@ -62,8 +51,10 @@ SCRATCH = {
     "P": ("sbuf", [128, 128], "float32"),
     "X": ("sbuf", [128, 128], "float32"),
     "Qi": ("sbuf", [128, 128], "int32"),
-    "cat": ("sbuf", [128, 48], "float32"),
-    "dl": ("sbuf", [128, 112], "float32"),
+    "cat": ("sbuf", [128, 64], "float32"),
+    "dl": ("sbuf", [128, 144], "float32"),
+    "e3": ("sbuf", [128, 16], "float32"),
+    "off": ("sbuf", [128, 8], "uint16"),
     "HD": ("sbuf", [128, 48], "float32"),
     "rt": ("sbuf", [128, 64], "float32"),
     "K": ("sbuf", [128, 32], "float32"),
@@ -74,6 +65,7 @@ SCRATCH = {
     "o13": ("sbuf", [128, 16], "uint16"),
     "o2": ("sbuf", [128, 8], "uint16"),
     "old": ("sbuf", [128, 128], "float32"),
+    "yh": ("sbuf", [128, 128], "float32"),
     "sm": ("sbuf", [128, 128], "int32"),
     "sn": ("sbuf", [128, 128], "int32"),
     "fin": ("sbuf", [128, 128], "float32"),
@@ -92,11 +84,11 @@ SEMAPHORES = (["qv", "qs", "qp", "qg", "sent", "ld0", "ld1", "ld2", "ld3", "st0"
               + ["e%d%s" % (i, h) for i in range(RO * 2) for h in ("", "a", "b")])
 
 PARTS = {"": (0, 128), "a": (0, 64), "b": (64, 128), "c": (0, 32), "d": (32, 64), "e": (64, 96), "f": (96, 128),
-         "g": (0, 96), "h": (32, 128)}
-ORDER = ("GA0a k vGA0b YA0 U0 K+P0 C0a+C0b L1 GS0 GA1a GA1b MA0 e1 vQ P1 YS0 MS0 "
-         "YA1a MA1a GS1 YA1b U1 MA1b D1 C1a+C1b L2 H GA2a GA2b YS1 h e2 MS1 P2 "
-         "YA2a MA2a GS2 YA2b U2 MA2b D2 C2a+C2b L3 GA3a GA3b X XX S j YS2 F MS2 FF GS3a GS3b YA3a vR MA3a YA3b x MA3b y "
-         "YS3a MS3a YS3b W MS3b w r J+Ja Jb Z")
+         "g": (0, 96), "h": (32, 128), "m": (0, 80), "n": (80, 128), "o": (0, 112), "p": (112, 128)}
+ORDER = ("GA0a B K Q vGA0b GS0 P0 YA0 U0 MA0 e1 C0a+C0b L1 G GA1a GA1b YS0 MS0 P1 "
+         "YA1a MA1a YA1b U1 MA1b GS1 D1 C1a+C1b L2 GA2a H GA2b S YS1 MS1 GS2 "
+         "YA2a MA2a P2 h e2 YA2b U2 MA2b D2 C2a+C2b L3 N GA3a GA3b YS2 F MS2 FF YA3a MA3a YA3b R GS3a GS3e i vGS3f u E "
+         "YS3f MS3f YS3a MS3a YS3e W MS3e w I:01 r I:12 MA3b EE ii I:23 Ja:01 I:34 T SS I:46 Ja:12 I:67 Ja:23 I:7a Jb:02 II Jb:23 Z")
 
 
 def rank_program(g, core, T, topo):
@@ -116,7 +108,7 @@ def rank_program(g, core, T, topo):
         for buf, lo, hi, w in [(o[1], o[2], o[3], True) for o in outs] + [(i[1], i[2], i[3], False) for i in ins]:
             for (lo2, hi2, w2, q2, s2, v2, c2) in log.get(buf, []):
                 if q2 == q:
-                    if not (w2 and (q != "p" or not w) and lo < hi2 and lo2 < hi):
+                    if q == "p" or not ((w or w2) and lo < hi2 and lo2 < hi):
                         continue
                 elif buf in PSUM:
                     pass
@@ -218,15 +210,15 @@ def rank_program(g, core, T, topo):
     def vgather(out, win, off):
         run("v", lambda: g.vector.tensor_copy(out[0], win[0].indirect(off[0])), [out], [win, off])
 
-    def sgather(out, win, off):
-        run("s", lambda: g.scalar.activation(out[0], win[0].indirect(off[0]), fn.Copy), [out], [win, off])
+    def sgather(out, win, off, scale=1.0, bias=0.0):
+        run("s", lambda: g.scalar.activation(out[0], win[0].indirect(off[0]), fn.Copy, bias=bias, scale=scale), [out], [win, off])
 
     def act(out, in_, scale=1.0, bias=0.0, f=None):
         ins = [in_] + [x for x in (scale, bias) if isinstance(x, tuple)]
         run("s", lambda: g.scalar.activation(out[0], in_[0], f or fn.Copy, bias=val(bias), scale=val(scale)), [out], ins)
 
-    def gadd(out, win, off, b):
-        run("v", lambda: g.vector.tensor_tensor(out[0], win[0].indirect(off[0]), b[0], op.add), [out], [win, off, b])
+    def gadd(out, win, off, b, o=op.add):
+        run("v", lambda: g.vector.tensor_tensor(out[0], win[0].indirect(off[0]), b[0], o), [out], [win, off, b])
 
     def scatter(win, off, in_):
         run("v", lambda: g.vector.tensor_copy(win[0].indirect(off[0]), in_[0]), [win], [in_, off])
@@ -241,6 +233,9 @@ def rank_program(g, core, T, topo):
     def iota(out, pattern, base, cm):
         kw = {} if SCRATCH[out[1]][2] == "int32" else {"allow_small_or_imprecise_dtypes": True}
         run("g", lambda: g.iota(out[0], pattern, base, cm, **kw), [out], [])
+
+    def select(out, in_, pattern, o, base, cm):
+        run("g", lambda: g.affine_select(out[0], in_[0], pattern, o, 0.0, base, cm), [out], [in_])
 
     n_eng = min(len(topo.engines(a, b)) for a in T.cores for b in T.cores if a != b)
     sends = [0]
@@ -266,58 +261,59 @@ def rank_program(g, core, T, topo):
 
     def send_reply(t, lo, hi, s):
         p = T.cores[(rank - 1 - t % (n_ranks - 1)) % n_ranks]
-        send(p, W("Eq", t * 32 + lo, t * 32 + hi), W("Er", t * 32 + lo, t * 32 + hi), s)
+        send(p, W("Eq", t * 48 + lo, t * 48 + hi), W("Er", t * 48 + lo, t * 48 + hi), s)
 
     dma("y", W("chI"), ext(T.ch[:, :]), "ld0")
-    dma("s", W("tab"), ext(T.xt[:, :]), "ld2")
-    dma("y", A("slI", rows=8), ext(T.sl[:, :]), "ld3")
-    dma("y", W("wI"), ext(T.wt[:, :]), "ld1")
+    dma("s", W("wI"), ext(T.wt[:, :]), "ld1")
+    dma("y", W("tab"), ext(T.xt[:, :]), "ld2")
+    dma("s", A("slI", rows=8), ext(T.sl[:, :]), "ld3")
+    def pair(name, n, x):
+        fill(A(name, 0, n), x)
+        fill(A(name, n, 2 * n), -x)
+
+    pair("big", 128, BIG)
     iota(A("kI", 0, 1), [[0, 1]], 0, 1)
-    iota(A("pf", 3, 4), [[0, 1]], 0, 16)
-    iota(A("rowb"), [[16, 8], [0, 16]], 0, 0)
-    iota(A("rowj"), [[1, 144]], -15, 0)
-    iota(A("rowx"), [[0, 8], [1, 16]], 0, 0)
-    iota(A("cKi"), [[4096, 4], [512, 8]], 0, 0)
     iota(A("kf", 4, 7), [[64 * 77, 3]], 0, 0)
-    fill(A("mx", 0, 1024), 1.0)
-    fill(A("neg"), -1.0)
-    fill(A("mx", 0, 1024, 16), 0.0)
-    ts(A("kI", 1, 2), A("kI", 0, 1), 112, None, op.bitwise_and)
-    ts(A("kI", 2, 3), A("kI", 0, 1), 15, None, op.bitwise_and)
-    fill(A("c32"), 1.0 / 32)
-    act(A("mx", 1024, 2048), A("mx", 0, 1024))
+    select(A("B2"), A("big"), [[0, 2], [-16, 8], [0, 16]], op.is_ge, 0, 1)
+    select(A("B2"), A("B2"), [[0, 2], [16, 8], [0, 16]], op.is_ge, 15, -1)
+    iota(A("rowx"), [[0, 8], [1, 16]], 0, 0)
+    fill(A("mx"), 1.0)
+    fill(A("mx", 0, 2048, 16), 0.0)
+    ts(A("kI", 1, 2), A("kI", 0, 1), 15, None, op.bitwise_and)
+    ts(A("kI", 2, 3), A("kI", 0, 1), 14, None, op.bitwise_and)
     act(A("mn"), A("mx"), -512.0, 512.0)
-    cp(A("pf", 0, 3), A("kI", 0, 3))
-    p_, blk_, k_, p16_ = [A("pf", n, n + 1) for n in range(4)]
-    ts(A("B8"), A("rowb"), p16_, BIG, op.is_equal, op.mult)
-    ts(A("Bp"), A("rowb"), blk_, None, op.is_equal)
-    ts(A("kf", 7, 8), k_, 64.0 * 613, -1048576.0, op.mult, op.add)
-    ts(A("Zp"), A("rowj"), blk_, None, op.is_equal)
-    ts(A("Ip"), A("rowj", 15, 143), p_, None, op.is_equal)
-    ts(A("Z8"), A("rowj"), p16_, None, op.is_equal)
-    ts(A("wf", 3, 4), k_, 32.0, None, op.mult)
-    ts(A("dt", 0, 128), A("rowx"), k_, -DG, op.is_lt, op.mult)
-    ts(A("dt", 128, 256), A("rowx"), k_, DG, op.is_equal, op.mult)
+    pair("one", 144, 1.0)
+    COLS = {"k": (1.0, 0.0), "8k": (8.0, 0.0), "-8k": (-8.0, 24.0), "613k": (64.0 * 613, -1048576.0),
+            "32k": (32.0, 0.0), "-k": (-1.0, 0.5), "lift": (DG, 2 * DG)}
+    col_ = {name: A("pf", n, n + 1) for n, name in enumerate(COLS)}
+    for name in ("k", "8k", "-8k", "613k"):
+        ts(col_[name], A("kI", 1, 2), COLS[name][0], COLS[name][1], op.mult, op.add)
     cp(A("L", 0, 128), A("chI"))
     send_list(0, 0)
-    tt(A("dm", 0, 128), A("dt", 0, 128), A("dt", 128, 256), op.add)
-    ts(A("cK"), A("cKi"), A("wf", 3, 4), None, op.add)
-    ts(A("kf", 0, 3), A("kf", 4, 7), A("kf", 7, 8), None, op.add)
-    ts(A("dm", 15, 128, 16), A("dm", 15, 128, 16), -2 * DG, None, op.add)
-    cp(A("slb", rows=8), A("slI", rows=8))
     for n, m in ((0, 4064), (1, 31)):
         ts(A("wq", n, n + 1), A("wI"), m, None, op.bitwise_and)
-    cp(A("wf", 0, 2), A("wq", 0, 2))
-    for name, src, x in (("Bb", "Bp", BIG), ("Bbn", "Bp", -BIG), ("Bn", "Bp", -1.0), ("Bh", "Bp", BIG / 2),
-                         ("Bhn", "Bp", -BIG / 2), ("In", "Ip", -1.0), ("Zn", "Zp", -1.0),
-                         ("Wh", "Bp", A("wf", 0, 1)), ("Wl", "Bp", A("wf", 1, 2)), ("Zw", "Zp", A("wf", 1, 2))):
-        act(A(name), A(src), x)
-    act(A("dm", 128, 256), A("dm", 0, 128))
+    ts(A("kf", 0, 3), A("kf", 4, 7), col_["613k"], None, op.add)
+    ts(A("wf", 0, 2), A("wq", 0, 2), 1.0 / BIG, None, op.mult)
+    cp(A("wf", 2, 3), A("wq", 1, 2))
+    ts(A("off", 0, 3), A("kf", 4, 7), 0.0, col_["k"], op.mult, op.add)
+    cp(A("off", 4, 5), A("kI", 2, 3))
+    ts(A("off", 6, 7), A("kI", 2, 3), -7.5, col_["8k"], op.mult, op.add)
+    ts(A("off", 7, 8), A("kI", 2, 3), 8.5, col_["-8k"], op.mult, op.add)
+    cp(A("slb", 0, 384, rows=8), A("slI", 0, 384, rows=8))
+    select(A("B8", rows=8), A("big", 0, 128, rows=8), [[1, 8], [0, 16]], op.is_equal, 0, -1)
+    iota(A("cKi", 0, 16), [[512, 8], [4096, 2]], 0, 0)
+    iota(A("cKi", 16, 32), [[512, 8], [-4096, 2]], 3 * 4096, 0)
+    select(A("Z8", rows=8), A("one", rows=8), [[0, 2], [1, 144]], op.is_equal, -15, -16)
+    select(A("Z2"), A("one"), [[0, 2], [0, 9], [1, 16]], op.is_equal, -15, 0)
+    select(A("Z2"), A("Z2"), [[0, 2], [-16, 9], [0, 16]], op.is_ge, 0, 1)
+    select(A("Z2"), A("Z2"), [[0, 2], [16, 9], [0, 16]], op.is_ge, 15, -1)
+    Bb, Bbn, Ip, In, neg = A("B2", 0, 128), A("B2", 128, 256), A("I2", 0, 128), A("I2", 144, 272), A("one", 144, 272)
 
-    def pick(name, k, rows=128):
-        return A(name, 15 - k, 143 - k, rows=rows)
+    def pick(name, k, minus=0, rows=128):
+        return A(name, 144 * minus + 15 - k, 144 * minus + 143 - k, rows=rows)
 
-    mm(A("pX", 0, 72), [(pick("Z8", k, 8), A("slb", k, 1152, 16, rows=8)) for k in range(16)])
+    def slack(t, j, k):
+        return A("slb", (t * 3 + j) * 128 + k, (t * 3 + j) * 128 + 128, 16, rows=8)
 
     def ends(name, c, lo=0, hi=128):
         return A(name, c * 2048 + 16 * lo + 15, c * 2048 + 16 * hi, 16)
@@ -352,35 +348,50 @@ def rank_program(g, core, T, topo):
             mm(H("pU"), [(A("Wh"), ends("YA", c, lo, hi)), (A("Wl"), ends("YA", c, lo, hi))])
         elif kind == "e":
             y0, m0 = ends("YA", 0, lo, hi), ends("MA", 0, lo, hi)
+            terms = [(Bb, y0), (Bbn, m0)]
             if c == 1:
-                terms = [(A("Bb"), y0), (A("Bbn"), m0)]
+                terms = terms + terms
             else:
-                terms = [(A("Bh"), y0), (A("Bhn"), m0), (A("Bh"), ends("YA", 1, lo, hi)), (A("Bhn"), ends("MA", 1, lo, hi)),
-                         (A("Bh"), H("hx"))]
-            terms += [(A("B8", rows=8), H("slb", (t * 3 + c - 1) * 128, 8)), (A("Bb"), H("c32"))]
+                terms += [(Bb, ends("YA", 1, lo, hi)), (Bbn, ends("MA", 1, lo, hi)), (Bb, H("hx"))]
+            terms += 2 * [(A("B8", rows=8), H("slb", (t * 3 + c - 1) * 128, 8))] + [(A("B8", rows=8), H("one", 0, 8))]
             mm(H("pD"), terms, True, False)
         elif kind == "D":
-            mm(H("pD"), [(A("Bbn"), ends("YA", c, lo, hi)), (A("Bb"), ends("MA", c, lo, hi))], False, True)
+            mm(H("pD"), 2 * [(Bbn, ends("YA", c, lo, hi))] + 2 * [(Bb, ends("MA", c, lo, hi))], False, True)
         elif kind == "H":
             act(A("sg"), A("pD", 0, 128), f=fn.Sign)
-            mm(A("pX", 128, 256), [(A("Ip"), ends("YA", 1)), (A("In"), ends("MA", 1)), (A("In"), ends("YA", 0)), (A("Ip"), ends("MA", 0))])
+            mm(A("pX", 128, 256), [(Ip, ends("YA", 1)), (In, ends("MA", 1)), (In, ends("YA", 0)), (Ip, ends("MA", 0))])
         elif kind == "h":
             tt(A("hx"), A("pX", 128, 256), A("sg"), op.mult)
-        elif kind == "S":
-            for d in range(2 if t == 0 else 0):
-                act(A("a8", d, 144, 2), A("pX", 0, 72))
-            for j in range(RO if t == 0 and "Jw" in ORDER else 0):
-                act(A("a8", 48 * j + 32, 48 * j + 48), A("a8", 48 * j + 32, 48 * j + 48), bias=-DG)
-        elif kind == "k":
-            if t > 0:
-                tt(A("rt", 48, 56), A("rt", 32, 40), A("rt", 24, 32), op.is_equal)
-                tt(A("r3"), A("rt", 48, 56), A("HD", 33, 48, 2), op.mult)
-                mm(A("pX", 256, 257), [(A("neg"), A("r3", n, n + 1)) for n in range(8)])
+        elif kind == "B":
+            if t == 0:
+                act(A("Wh"), Bb, A("wf", 0, 1))
+                act(A("Wl"), Bb, A("wf", 1, 2))
+                for name in ("-k", "32k", "lift"):
+                    act(col_[name], col_["k"], COLS[name][0], COLS[name][1])
+                act(A("dm"), A("rowx"), bias=col_["-k"], f=fn.Sign)
+                act(A("dm"), A("dm"), DG)
+                act(A("dm", 15, 128, 16), A("dm", 15, 128, 16), bias=-18 * DG)
+        elif kind == "G":
+            if t == 0:
+                select(A("I2"), A("one"), [[0, 2], [-1, 144]], op.is_equal, 0, 1)
+                iota(A("Er"), [[0, RO * 48]], 0, 0)
+                iota(A("cat", 48, 64), [[0, 16]], 0, 0)
+        elif kind == "T":
+            if t + 1 < RO:
+                cp(A("slb", 384 * t + 384, 384 * t + 768, rows=8), A("slI", 384 * t + 384, 384 * t + 768, rows=8))
+        elif kind in ("S", "SS"):
+            u = t + (kind == "SS")
+            if u < RO and (kind == "SS" or t == 0):
+                if kind == "S":
+                    act(A("Zw"), A("Z2", 0, 144), A("wf", 2, 3))
+                    act(A("cK"), A("cKi"), bias=col_["32k"], f=fn.Identity)
+                for j in range(2):
+                    mm(A("pY", 32 + 8 * j, 40 + 8 * j), [(pick("Z8", k, 1 - j, 8), slack(u, j, k)) for k in range(16)])
+                for d in range(2):
+                    act(A("a8", 32 * u + d, 32 * u + 32, 2), A("pY", 32, 48))
         elif kind == "K":
             if t > 0:
-                cp(A("kq", 0, 1), A("pX", 256, 257))
-                ts(A("kq", 1, 2), A("kq", 0, 1), 31, None, op.bitwise_and)
-                ts(A("kf", 0, 1), A("kq", 1, 2), 64.0, A("kf", 7, 8), op.mult, op.add)
+                ts(A("kf", 0, 1), A("kq", 1, 2), 64.0, col_["613k"], op.mult, op.add)
         elif kind == "Q":
             if t > 0:
                 if onv:
@@ -407,120 +418,125 @@ def rank_program(g, core, T, topo):
             ts(H("L", (i + 1) * 128), H("NW", (c + 1) * 128), 1.0 / 64, None, op.mult)
         elif kind == "L":
             send_list(t, c, h)
-        elif kind == "X":
-            mm(A("pC", 0, 24), [(pick("Zp", k), col("YA", k, 0, 3)) for k in range(16)], True, False)
-        elif kind == "XX":
-            mm(A("pC", 0, 24), [(pick("Zn", k), col("MA", k, 0, 3)) for k in range(16)], False, True)
-        elif kind == "x":
-            mm(A("pZ", 8, 40), [(pick("Zw", k), col("YA", k, 0, 4)) for k in range(16)])
-            mm(A("pZ", 0, 8), [(pick("Zp", k), col("YA", k, 3, 4)) for k in range(16)], True, False)
-        elif kind == "y":
-            mm(A("pZ", 0, 8), [(pick("Zn", k), col("MA", k, 3, 4)) for k in range(16)], False, True)
+        elif kind == "N":
+            mm(A("pC", 0, 24), [(pick("Z2", k), col("YA", k, 0, 3)) for k in range(16)]
+               + [(pick("Z2", k, 1), col("MA", k, 0, 3)) for k in range(16)])
+        elif kind == "E":
+            mm(A("pX", 80, 88), [(pick("Z8", k, 1, 8), slack(t, 2, k)) for k in range(16)]
+               + [(pick("Z2", k), col("YA", k, 3, 4)) for k in range(16)], True, False)
+        elif kind == "EE":
+            mm(A("pX", 80, 88), [(pick("Z2", k, 1), col("MA", k, 3, 4)) for k in range(16)], False, True)
+        elif kind == "i":
+            (cp if onv else act)(A("cat", 0, 48, 2), A("pC", 0, 24))
+        elif kind == "ii":
+            for d in range(2):
+                act(A("e3", d, 16, 2), A("pX", 80, 88))
+        elif kind == "I":
+            n0, m0, d1, t1, m1, s2 = [W("dl", 16 * n, 16 * n + 16) for n in (0, 3, 4, 5, 6, 8)]
+            a0, a1 = [A("a8", (t * 2 + j) * 16, (t * 2 + j) * 16 + 16) for j in range(2)]
+            tt(A("cat", 1, 48, 2), A("pC", 0, 24), A("Eq", t * 48, t * 48 + 24), op.add)
+            gadd(W("dl", 0, 48), W("cat", 0, 16), W("off", 0, 3), W("cat", 16, 64), op.subtract)
+            tt(A("HD", 0, 16), n0, a0, op.is_ge)
+            tt(m0, n0, A("HD", 0, 16), op.mult)
+            gadd(W("dl", 64, 96), m0, W("off", 0, 2), W("dl", 16, 48), op.subtract)
+            tt(A("HD", 16, 32), d1, a1, op.is_le)
+            tt(m1, d1, A("HD", 16, 32), op.mult)
+            tt(s2, t1, m1, op.subtract)
+            tt(A("HD", 0, 32, 2), A("HD", 0, 32, 2), A("HD", 1, 32, 2), op.is_equal)
+            gadd(W("HD", 16, 32), W("HD", 0, 16), W("off", 4, 5), W("HD", 16, 32), op.mult)
+        elif kind == "II":
+            tt(A("dl", 112, 128), A("dl", 128, 144), A("e3"), op.add)
         elif kind == "u":
-            mm(A("pC", 24, 48), [(pick("Zw", k), col("YA", k, 0, 3)) for k in range(16)])
-        elif kind == "xw":
-            mm(A("pZ", 128, 256), [(A("Wl"), ends("YA", 3))])
-            mm(A("pZ", 0, 128), [(A("Bp"), ends("YA", 3))], True, False)
-        elif kind == "yw":
-            mm(A("pZ", 0, 128), [(A("Bn"), ends("MA", 3))], False, True)
-        elif kind == "Jw":
-            scan(A("dz"), A("pZ", 0, 256), A("dm"), op.max, op.add)
-            cp(A("Ki", 0, 24), A("pC", 24, 48))
-            ts(A("Ki", 24, 32), A("dz", 128 + 15, 256, 16), DG, None, op.add)
-            tt(A("rt", 16, 24), A("dl", 97, 112, 2), A("dz", 15, 128, 16), op.subtract)
-            ts(A("Ki", 32, 64), A("Ki", 0, 32), 31, None, op.bitwise_and)
-            tt(A("rt", 24, 32), A("dz", 15, 128, 16), A("dl", 96, 112, 2), op.is_le)
-            tt(A("K"), A("Ki", 32, 64), A("cK"), op.add)
-            tt(A("cf", 0, 24), A("HD", 1, 48, 2), A("K", 8, 32), op.mult)
-            tt(A("cf", 24, 32), A("K", 0, 8), A("cf", 0, 8), op.max)
-            tt(A("cf", 32, 40), A("cf", 24, 32), A("cf", 8, 16), op.max)
+            mm(A("pZ", 0, 32), [(pick("Zw", k), col("YA", k, 0, 4)) for k in range(16)])
         elif kind == "Ja":
-            cp(A("Ki", 0, 32), A("pZ", 8, 40))
+            cp(A("Ki", 0, 32), A("pZ", 0, 32))
             ts(A("Ki", 32, 64), A("Ki", 0, 32), 31, None, op.bitwise_and)
-            tt(A("K"), A("Ki", 32, 64), A("cK"), op.add)
-        elif kind == "Jb":
-            tt(A("cf", 0, 24), A("HD", 1, 48, 2), A("K", 8, 32), op.mult)
-            tt(A("rt", 16, 24), A("dl", 97, 112, 2), A("pZ", 0, 8), op.subtract)
-            tt(A("cf", 24, 32), A("K", 0, 8), A("cf", 0, 8), op.max)
-            tt(A("rt", 24, 32), A("pZ", 0, 8), A("dl", 96, 112, 2), op.is_le)
-            tt(A("cf", 32, 40), A("cf", 24, 32), A("cf", 8, 16), op.max)
+            gadd(W("K"), W("Ki", 32, 64), W("off", 6, 8), W("cK"))
         elif kind == "F":
-            mm(A("pY", 0, 24), [(pick("Zp", k), col("YS", k, 0, 3)) for k in range(16)], True, False)
+            mm(A("pY", 0, 24), [(pick("Z2", k), col("YS", k, 0, 3)) for k in range(16)], True, False)
         elif kind == "FF":
-            mm(A("pY", 0, 24), [(pick("Zn", k), col("MS", k, 0, 3)) for k in range(16)], False, True)
+            mm(A("pY", 0, 24), [(pick("Z2", k, 1), col("MS", k, 0, 3)) for k in range(16)], False, True)
         elif kind == "R":
-            (cp if onv else act)(A("Er", t * 32, t * 32 + 24), A("pY", 0, 24))
+            (cp if onv else act)(A("Er", t * 48, t * 48 + 24), A("pY", 0, 24))
             send_reply(t, 0, 24, "e%d" % (2 * t))
         elif kind == "W":
-            mm(H("pW"), [(A("Bp"), ends("YS", 3, lo, hi))], True, False)
+            mm(H("pW"), [(Bb, ends("YS", 3, lo, hi))], True, False)
         elif kind == "w":
-            mm(H("pW"), [(A("Bn"), ends("MS", 3, lo, hi))], False, True)
+            mm(H("pW"), [(Bbn, ends("MS", 3, lo, hi))], False, True)
         elif kind == "r":
             scan(H("dg"), H("pW"), H("dm"), op.max, op.add)
-            ts(A("Er", t * 32 + 24 + lo // 16, t * 32 + 24 + hi // 16), A("dg", lo + 15, hi, 16), DG, None, op.add)
-            send_reply(t, 24 + lo // 16, 24 + hi // 16, "e%d%s" % (2 * t + 1, h))
-        elif kind == "j":
-            (cp if onv else act)(A("cat", 0, 48, 2), A("pC", 0, 24))
-        elif kind == "J":
-            tt(A("cat", 1, 48, 2), A("pC", 0, 24), A("Eq", t * 32, t * 32 + 24), op.add)
-            st = A("cat", 0, 16)
-            for j in range(2):
-                a = (t * 3 + j) * 16
-                d, m, nx = [A("dl", 48 * j + 16 * n, 48 * j + 16 * n + 16) for n in range(3)]
-                tt(d, A("cat", 16 * j + 16, 16 * j + 32), st, op.subtract)
-                tt(A("HD", 16 * j, 16 * j + 16), d, A("a8", a, a + 16), op.is_le)
-                tt(m, d, A("HD", 16 * j, 16 * j + 16), op.mult)
-                tt(nx, st, m, op.add)
-                st = nx
-            a = (t * 3 + 2) * 16
-            tt(A("rt", 0, 16), A("HD", 0, 32, 2), A("HD", 1, 32, 2), op.is_equal)
-            tt(A("dl", 96, 112), st, A("a8", a, a + 16), op.add)
-            tt(A("HD", 33, 48, 2), A("rt", 0, 8), A("rt", 8, 16), op.mult)
-            tt(A("HD", 17, 32, 2), A("HD", 17, 32, 2), A("rt", 0, 8), op.mult)
-        elif kind == "Jk":
-            cp(A("Ki", 0, 32), A("pZ", 8, 40))
-            tt(A("rt", 16, 24), A("dl", 97, 112, 2), A("pZ", 0, 8), op.subtract)
-            ts(A("Ki", 32, 64), A("Ki", 0, 32), 31, None, op.bitwise_and)
-            tt(A("rt", 24, 32), A("pZ", 0, 8), A("dl", 96, 112, 2), op.is_le)
-            tt(A("K"), A("Ki", 32, 64), A("cK"), op.add)
-            tt(A("cf", 0, 24), A("HD", 1, 48, 2), A("K", 8, 32), op.mult)
-            tt(A("cf", 24, 32), A("K", 0, 8), A("cf", 0, 8), op.max)
-            tt(A("cf", 32, 40), A("cf", 24, 32), A("cf", 8, 16), op.max)
+            ts(A("Er", t * 48 + 33 + lo // 8, t * 48 + 32 + hi // 8, 2), A("dg", lo + 15, hi, 16), col_["lift"], -1.0 / BIG,
+               op.add, op.mult)
+            send_reply(t, 32 + lo // 8, 32 + hi // 8, "e%d%s" % (2 * t + 1, h))
+        elif kind == "Jb":
+            tt(A("cf", 0, 32), A("HD", 0, 32), A("K"), op.mult)
+            tt(A("cf", 32, 40), A("K", 0, 16, 2), A("cf", 1, 16, 2), op.max)
+            tt(A("cf", 40, 48), A("cf", 32, 40), A("cf", 17, 32, 2), op.max)
         elif kind == "Z":
             last = t == RO - 1
-            n = t * 32 + 24
-            tt(A("rt", 32, 40), A("Eq", n, n + 8), A("rt", 16, 24), op.is_le)
-            tt(A("rt", 40, 48), A("rt", 32, 40), A("cf", 16, 24), op.mult)
-            tt(A("ci", 0, 8), A("rt", 40, 48), A("cf", 32, 40), op.max)
+            n = t * 48 + 32
+            tt(A("HD", 32, 48), A("dl", 112, 128), A("Eq", n, n + 16), op.is_le)
+            tt(A("rt", 0, 8), A("HD", 33, 48, 2), A("cf", 16, 32, 2), op.mult)
+            if not last:
+                tt(A("rt", 8, 16), A("HD", 32, 48, 2), A("HD", 33, 48, 2), op.is_equal)
+            tt(A("ci", 0, 8), A("rt", 0, 8), A("cf", 40, 48), op.max)
+            if not last:
+                tt(A("r3"), A("rt", 8, 16), A("HD", 16, 32, 2), op.mult)
+                mm(A("pX", 256, 257), [(neg, A("r3", n, n + 1)) for n in range(8)])
             ts(A("ci", 8, 16), A("ci", 0, 8), 5, None, op.arith_shift_right)
-            if last:
-                ts(A("ci", 16, 24), A("ci", 0, 8), 2047, None, op.bitwise_and)
-            else:
-                ts(A("ci", 16, 24), A("ci", 0, 8), 4095, None, op.bitwise_and)
+            ts(A("ci", 16, 24), A("ci", 0, 8), 2047 if last else 4095, None, op.bitwise_and)
             cp(A("o13"), A("ci", 8, 24))
             o1 = W("o13", 0, 8)
-            parts = [(0, 64), (64, 128)] if last else [(0, 128)]
-            for a, b in parts:
-                sgather(W("old", a, b), W("tab", 32 * a, 32 * b), W("o13", 8 + a // 16, 8 + b // 16))
+
+            def o3(a, b):
+                return W("o13", 8 + a // 16, 8 + b // 16)
+
+            def mean(a, b):
+                gadd(W("sm", a, b), W("YA"), W("o2", a // 16, b // 16), W("old", a, b))
+
+            def down(a, b):
+                ts(A("sn", a, b), A("sm", a, b), 1, None, op.arith_shift_right)
+
+            def put(a, b):
+                scatter(W("tab", 32 * a, 32 * b), o3(a, b), W("sn", a, b))
+
             if not last:
                 nxt = (t + 1) * NL * 128
+                sgather(W("old"), W("tab"), o3(0, 128), 0.5, -0.25)
+                ts(A("o2"), o1, 16.0, 15.0, op.mult, op.add)
+                sgather(W("yh"), W("YA"), W("o2"), 0.5)
                 ts(W("L", nxt, nxt + 128), W("NW"), 1.0 / 64, None, op.mult, off=o1)
                 send_list(t + 1, 0)
-            ts(A("o2"), o1, 16.0, 15.0, op.mult, op.add)
-            for a, b in parts:
-                gadd(W("sm", a, b), W("YA"), W("o2", a // 16, b // 16), W("old", a, b))
-                ts(A("sn", a, b), A("sm", a, b), 1, None, op.arith_shift_right)
-                win = W("tab", 32 * a, 32 * b)
-                scatter(win, W("o13", 8 + a // 16, 8 + b // 16), W("sn", a, b))
-                if last:
-                    dma("y" if a == 0 else "s", ext(T.yx[:, 32 * a:32 * b]), win, "st0" if a == 0 else "st1")
-            if last:
+                cp(A("kq", 0, 1), A("pX", 256, 257))
+                tt(A("sn"), A("old"), A("yh"), op.add)
+                ts(A("kq", 1, 2), A("kq", 0, 1), 31, None, op.bitwise_and)
+                put(0, 128)
+            else:
+                for a, b in ((0, 64), (64, 128)):
+                    sgather(W("old", a, b), W("tab", 32 * a, 32 * b), o3(a, b))
+                ts(A("o2"), o1, 16.0, 15.0, op.mult, op.add)
                 ts(W("fin"), W("NW"), 1.0 / 64, None, op.mult, off=o1)
                 dma("y", ext(T.yc[:, :]), W("fin"), "st2")
+                mean(0, 64)
+                mean(64, 128)
+                down(0, 64)
+                down(64, 128)
+                put(0, 64)
+                dma("y", ext(T.yx[:, 0:2048]), W("tab", 0, 2048), "st0")
+                put(64, 128)
+                dma("s", ext(T.yx[:, 2048:4096]), W("tab", 2048, 4096), "st1")
 
     issue(taken())
     for t in range(RO):
+        held = {}
         for w in ORDER.split():
+            if ":" in w:
+                x, n = w.split(":")
+                if x not in held:
+                    piece(t, x)
+                    held[x] = taken()
+                issue(held[x][int(n[0], 36):int(n[1], 36)])
+                continue
             chains = []
             for x in w.split("+"):
                 for y in x.split("."):

from concourse.mybir import AluOpType, ActivationFunctionType

RO, NL = 3, 4
BIG = 2.0 ** 25
DG = BIG * 2.0 ** 13
SCRATCH = {
    "tab": ("sbuf", [128, 4096], "bfloat16"),
    "chI": ("sbuf", [128, 128], "int32"),
    "NW": ("sbuf", [128, 512], "int32"),
    "L": ("sbuf", [128, RO * NL * 128], "uint16"),
    "Lr": ("sbuf", [128, RO * NL * 128], "uint16"),
    "gA": ("sbuf", [128, 8192], "bfloat16"),
    "gS": ("sbuf", [128, 8192], "bfloat16"),
    "YA": ("sbuf", [128, 8192], "bfloat16"),
    "MA": ("sbuf", [128, 8192], "bfloat16"),
    "YS": ("sbuf", [128, 8192], "bfloat16"),
    "MS": ("sbuf", [128, 8192], "bfloat16"),
    "Er": ("sbuf", [128, RO * 48], "float32"),
    "Eq": ("sbuf", [128, RO * 48], "float32"),
    "mx": ("sbuf", [128, 2048], "bfloat16"),
    "mn": ("sbuf", [128, 2048], "bfloat16"),
    "rowx": ("sbuf", [128, 128], "float32"),
    "dm": ("sbuf", [128, 128], "float32"),
    "dg": ("sbuf", [128, 128], "float32"),
    "big": ("sbuf", [128, 256], "bfloat16"),
    "one": ("sbuf", [128, 288], "bfloat16"),
    "B2": ("sbuf", [128, 256], "bfloat16"),
    "B8": ("sbuf", [128, 128], "bfloat16"),
    "Wh": ("sbuf", [128, 128], "bfloat16"),
    "Wl": ("sbuf", [128, 128], "bfloat16"),
    "I2": ("sbuf", [128, 288], "bfloat16"),
    "sg": ("sbuf", [128, 128], "bfloat16"),
    "hx": ("sbuf", [128, 128], "bfloat16"),
    "Z2": ("sbuf", [128, 288], "bfloat16"),
    "Zw": ("sbuf", [128, 144], "bfloat16"),
    "Z8": ("sbuf", [128, 288], "bfloat16"),
    "slI": ("sbuf", [128, 1152], "int32"),
    "slb": ("sbuf", [128, 1152], "bfloat16"),
    "a8": ("sbuf", [128, RO * 32], "float32"),
    "wI": ("sbuf", [128, 1], "int32"),
    "wq": ("sbuf", [128, 4], "int32"),
    "wf": ("sbuf", [128, 4], "float32"),
    "kI": ("sbuf", [128, 4], "int32"),
    "pf": ("sbuf", [128, 8], "float32"),
    "kf": ("sbuf", [128, 8], "float32"),
    "kq": ("sbuf", [128, 2], "int32"),
    "cKi": ("sbuf", [128, 32], "float32"),
    "cK": ("sbuf", [128, 32], "float32"),
    "Ui": ("sbuf", [128, 128], "int32"),
    "ua": ("sbuf", [128, 128], "int32"),
    "P": ("sbuf", [128, 128], "float32"),
    "X": ("sbuf", [128, 128], "float32"),
    "Qi": ("sbuf", [128, 128], "int32"),
    "cat": ("sbuf", [128, 64], "float32"),
    "dl": ("sbuf", [128, 144], "float32"),
    "e3": ("sbuf", [128, 16], "float32"),
    "off": ("sbuf", [128, 8], "uint16"),
    "HD": ("sbuf", [128, 48], "float32"),
    "rt": ("sbuf", [128, 64], "float32"),
    "K": ("sbuf", [128, 32], "float32"),
    "Ki": ("sbuf", [128, 64], "int32"),
    "ci": ("sbuf", [128, 32], "int32"),
    "cf": ("sbuf", [128, 48], "float32"),
    "r3": ("sbuf", [128, 8], "bfloat16"),
    "o13": ("sbuf", [128, 16], "uint16"),
    "o2": ("sbuf", [128, 8], "uint16"),
    "old": ("sbuf", [128, 128], "float32"),
    "yh": ("sbuf", [128, 128], "float32"),
    "sm": ("sbuf", [128, 128], "int32"),
    "sn": ("sbuf", [128, 128], "int32"),
    "fin": ("sbuf", [128, 128], "float32"),
    "pU": ("psum", [128, 512], "float32"),
    "pD": ("psum", [128, 512], "float32"),
    "pV": ("psum", [128, 512], "float32"),
    "pX": ("psum", [128, 512], "float32"),
    "pC": ("psum", [128, 512], "float32"),
    "pZ": ("psum", [128, 512], "float32"),
    "pY": ("psum", [128, 512], "float32"),
    "pW": ("psum", [128, 512], "float32"),
}
PSUM = [n for n in SCRATCH if SCRATCH[n][0] == "psum"]
SEMAPHORES = (["qv", "qs", "qp", "qg", "sent", "ld0", "ld1", "ld2", "ld3", "st0", "st1", "st2"]
              + ["l%d%s" % (i, h) for i in range(RO * NL) for h in ("", "a", "b")]
              + ["e%d%s" % (i, h) for i in range(RO * 2) for h in ("", "a", "b")])

PARTS = {"": (0, 128), "a": (0, 64), "b": (64, 128), "c": (0, 32), "d": (32, 64), "e": (64, 96), "f": (96, 128),
         "g": (0, 96), "h": (32, 128), "m": (0, 80), "n": (80, 128), "o": (0, 112), "p": (112, 128)}
ORDER = ("GA0a B K Q vGA0b GS0 P0 YA0 U0 MA0 e1 C0a+C0b L1 G GA1a GA1b YS0 MS0 P1 "
         "YA1a MA1a YA1b U1 MA1b GS1 D1 C1a+C1b L2 GA2a H GA2b S YS1 MS1 GS2 "
         "YA2a MA2a P2 h e2 YA2b U2 MA2b D2 C2a+C2b L3 N GA3a GA3b YS2 F MS2 FF YA3a MA3a YA3b R GS3a GS3e i vGS3f u E "
         "YS3f MS3f YS3a MS3a YS3e W MS3e w I:01 r I:12 MA3b EE ii I:23 Ja:01 I:34 T SS I:46 Ja:12 I:67 Ja:23 I:7a Jb:02 II Jb:23 Z")


def rank_program(g, core, T, topo):
    rank = T.rank_of(core)
    if rank is None:
        return
    op = AluOpType
    fn = ActivationFunctionType
    n_ranks = len(T.cores)
    Q = {"g": g, "v": g.vector, "s": g.scalar, "p": g.tensor, "y": g.sync}
    cnt = {"v": 0, "s": 0, "p": 0, "g": 0}
    known = {"g": {}, "v": {}, "s": {}, "p": {}, "y": {}}
    log = {}

    def need(q, outs, ins):
        evs = []
        for buf, lo, hi, w in [(o[1], o[2], o[3], True) for o in outs] + [(i[1], i[2], i[3], False) for i in ins]:
            for (lo2, hi2, w2, q2, s2, v2, c2) in log.get(buf, []):
                if q2 == q:
                    if q == "p" or not ((w or w2) and lo < hi2 and lo2 < hi):
                        continue
                elif buf in PSUM:
                    pass
                elif not ((w or w2) and lo < hi2 and lo2 < hi):
                    continue
                evs.append((s2, v2, c2))
        best = {}
        for s2, v2, c2 in evs:
            if known[q].get(s2, 0) < v2 and (s2 not in best or best[s2][0] < v2):
                best[s2] = (v2, c2)
        for s2 in list(best):
            if any(s3 != s2 and best[s3][1].get(s2, 0) >= best[s2][0] for s3 in best):
                continue
            v2, c2 = best[s2]
            Q[q].wait_ge(T.sem[s2], v2)
        for s2 in best:
            v2, c2 = best[s2]
            for s3 in c2:
                known[q][s3] = max(known[q].get(s3, 0), c2[s3])
            known[q][s2] = max(known[q].get(s2, 0), v2)

    def note(q, outs, ins, s, v, clock):
        for o in outs:
            log[o[1]] = [a for a in log.get(o[1], []) if not (o[2] <= a[0] and a[1] <= o[3])]
            log[o[1]].append((o[2], o[3], True, q, s, v, clock))
        for i in ins:
            log.setdefault(i[1], [])
            log[i[1]] = [a for a in log[i[1]] if a[2] or a[3] != q or not (i[2] <= a[0] and a[1] <= i[3])]
            log[i[1]].append((i[2], i[3], False, q, s, v, clock))

    jobs = []

    def run(q, call, outs, ins):
        def job():
            need(q, outs, ins)
            cnt[q] += 1
            call().then_inc(T.sem["q" + q], 1)
            clock = dict(known[q])
            clock["q" + q] = cnt[q]
            note(q, outs, ins, "q" + q, cnt[q], clock)
        jobs.append(job)

    def dma(q, out, in_, s):
        def job():
            o = [out] if out[1] else []
            i = [in_] if in_[1] else []
            need(q, o, i)
            Q[q].dma_start(out[0], in_[0]).then_inc(T.sem[s], 16)
            note("dma", o, i, s, 16, dict(known[q]))
        jobs.append(job)

    def issue(*lists):
        for n in range(max(len(x) for x in lists)):
            for x in lists:
                if n < len(x):
                    x[n]()

    def taken():
        x = list(jobs)
        del jobs[:]
        return x

    def ext(ap):
        return (ap, None, 0, 0)

    def A(name, lo=0, hi=None, st=1, rows=128):
        if hi is None:
            hi = SCRATCH[name][1][1]
        t = T[name]
        return (t[0:rows, lo:hi] if st == 1 else t[0:rows, lo:hi:st], name, lo, hi)

    def W(name, lo=0, hi=None):
        hi = SCRATCH[name][1][1] if hi is None else hi
        return (T[name][:, lo:hi], name, lo, hi)

    def val(x):
        return x[0] if isinstance(x, tuple) else x

    def cp(out, in_):
        run("v", lambda: g.vector.tensor_copy(out[0], in_[0]), [out], [in_])

    def tt(out, a, b, o):
        run("v", lambda: g.vector.tensor_tensor(out[0], a[0], b[0], o), [out], [a, b])

    def ts(out, a, s1, s2, o1, o2=None, off=None):
        ins = [a] + [s for s in (s1, s2, off) if isinstance(s, tuple)]
        x = a[0] if off is None else a[0].indirect(off[0])
        if o2 is None:
            run("v", lambda: g.vector.tensor_scalar(out[0], x, val(s1), None, o1), [out], ins)
        else:
            run("v", lambda: g.vector.tensor_scalar(out[0], x, val(s1), val(s2), o1, o2), [out], ins)

    def fill(out, c):
        run("v", lambda: g.vector.memset(out[0], c), [out], [])

    def scan(out, d0, d1, o0, o1):
        run("v", lambda: g.vector.tensor_tensor_scan(out[0], d0[0], d1[0], 0.0, o0, o1), [out], [d0, d1])

    def vgather(out, win, off):
        run("v", lambda: g.vector.tensor_copy(out[0], win[0].indirect(off[0])), [out], [win, off])

    def sgather(out, win, off, scale=1.0, bias=0.0):
        run("s", lambda: g.scalar.activation(out[0], win[0].indirect(off[0]), fn.Copy, bias=bias, scale=scale), [out], [win, off])

    def act(out, in_, scale=1.0, bias=0.0, f=None):
        ins = [in_] + [x for x in (scale, bias) if isinstance(x, tuple)]
        run("s", lambda: g.scalar.activation(out[0], in_[0], f or fn.Copy, bias=val(bias), scale=val(scale)), [out], ins)

    def gadd(out, win, off, b, o=op.add):
        run("v", lambda: g.vector.tensor_tensor(out[0], win[0].indirect(off[0]), b[0], o), [out], [win, off, b])

    def scatter(win, off, in_):
        run("v", lambda: g.vector.tensor_copy(win[0].indirect(off[0]), in_[0]), [win], [in_, off])

    def mm1(out, l, r, st, sp):
        run("p", lambda: g.tensor.matmul(out[0], l[0], r[0], st, sp), [out], [l, r])

    def mm(out, pairs, first=True, last=True):
        for n, (l, r) in enumerate(pairs):
            mm1(out, l, r, first and n == 0, last and n == len(pairs) - 1)

    def iota(out, pattern, base, cm):
        kw = {} if SCRATCH[out[1]][2] == "int32" else {"allow_small_or_imprecise_dtypes": True}
        run("g", lambda: g.iota(out[0], pattern, base, cm, **kw), [out], [])

    def select(out, in_, pattern, o, base, cm):
        run("g", lambda: g.affine_select(out[0], in_[0], pattern, o, 0.0, base, cm), [out], [in_])

    n_eng = min(len(topo.engines(a, b)) for a in T.cores for b in T.cores if a != b)
    sends = [0]

    def send(dst, out, in_, s):
        def job():
            need("g", [], [in_])
            rid, pid, _ = topo.addr(dst)
            m = sum(1 << e for e in topo.engines(core, dst)[:n_eng])
            g.remote_dma(out[0], in_[0], T.sem[s], T.sem.sent, pid, rid, m)
            sends[0] += n_eng
            note("x", [out], [], s, n_eng, {})
        jobs.append(job)

    def half(x):
        return PARTS[x]

    def send_list(t, c, h=""):
        i = t * NL + c
        lo, hi = half(h)
        q = T.cores[(rank + 1 + t % (n_ranks - 1)) % n_ranks]
        send(q, W("Lr", i * 128 + lo, i * 128 + hi), W("L", i * 128 + lo, i * 128 + hi), "l%d%s" % (i, h))

    def send_reply(t, lo, hi, s):
        p = T.cores[(rank - 1 - t % (n_ranks - 1)) % n_ranks]
        send(p, W("Eq", t * 48 + lo, t * 48 + hi), W("Er", t * 48 + lo, t * 48 + hi), s)

    dma("y", W("chI"), ext(T.ch[:, :]), "ld0")
    dma("s", W("wI"), ext(T.wt[:, :]), "ld1")
    dma("y", W("tab"), ext(T.xt[:, :]), "ld2")
    dma("s", A("slI", rows=8), ext(T.sl[:, :]), "ld3")
    def pair(name, n, x):
        fill(A(name, 0, n), x)
        fill(A(name, n, 2 * n), -x)

    pair("big", 128, BIG)
    iota(A("kI", 0, 1), [[0, 1]], 0, 1)
    iota(A("kf", 4, 7), [[64 * 77, 3]], 0, 0)
    select(A("B2"), A("big"), [[0, 2], [-16, 8], [0, 16]], op.is_ge, 0, 1)
    select(A("B2"), A("B2"), [[0, 2], [16, 8], [0, 16]], op.is_ge, 15, -1)
    iota(A("rowx"), [[0, 8], [1, 16]], 0, 0)
    fill(A("mx"), 1.0)
    fill(A("mx", 0, 2048, 16), 0.0)
    ts(A("kI", 1, 2), A("kI", 0, 1), 15, None, op.bitwise_and)
    ts(A("kI", 2, 3), A("kI", 0, 1), 14, None, op.bitwise_and)
    act(A("mn"), A("mx"), -512.0, 512.0)
    pair("one", 144, 1.0)
    COLS = {"k": (1.0, 0.0), "8k": (8.0, 0.0), "-8k": (-8.0, 24.0), "613k": (64.0 * 613, -1048576.0),
            "32k": (32.0, 0.0), "-k": (-1.0, 0.5), "lift": (DG, 2 * DG)}
    col_ = {name: A("pf", n, n + 1) for n, name in enumerate(COLS)}
    for name in ("k", "8k", "-8k", "613k"):
        ts(col_[name], A("kI", 1, 2), COLS[name][0], COLS[name][1], op.mult, op.add)
    cp(A("L", 0, 128), A("chI"))
    send_list(0, 0)
    for n, m in ((0, 4064), (1, 31)):
        ts(A("wq", n, n + 1), A("wI"), m, None, op.bitwise_and)
    ts(A("kf", 0, 3), A("kf", 4, 7), col_["613k"], None, op.add)
    ts(A("wf", 0, 2), A("wq", 0, 2), 1.0 / BIG, None, op.mult)
    cp(A("wf", 2, 3), A("wq", 1, 2))
    ts(A("off", 0, 3), A("kf", 4, 7), 0.0, col_["k"], op.mult, op.add)
    cp(A("off", 4, 5), A("kI", 2, 3))
    ts(A("off", 6, 7), A("kI", 2, 3), -7.5, col_["8k"], op.mult, op.add)
    ts(A("off", 7, 8), A("kI", 2, 3), 8.5, col_["-8k"], op.mult, op.add)
    cp(A("slb", 0, 384, rows=8), A("slI", 0, 384, rows=8))
    select(A("B8", rows=8), A("big", 0, 128, rows=8), [[1, 8], [0, 16]], op.is_equal, 0, -1)
    iota(A("cKi", 0, 16), [[512, 8], [4096, 2]], 0, 0)
    iota(A("cKi", 16, 32), [[512, 8], [-4096, 2]], 3 * 4096, 0)
    select(A("Z8", rows=8), A("one", rows=8), [[0, 2], [1, 144]], op.is_equal, -15, -16)
    select(A("Z2"), A("one"), [[0, 2], [0, 9], [1, 16]], op.is_equal, -15, 0)
    select(A("Z2"), A("Z2"), [[0, 2], [-16, 9], [0, 16]], op.is_ge, 0, 1)
    select(A("Z2"), A("Z2"), [[0, 2], [16, 9], [0, 16]], op.is_ge, 15, -1)
    Bb, Bbn, Ip, In, neg = A("B2", 0, 128), A("B2", 128, 256), A("I2", 0, 128), A("I2", 144, 272), A("one", 144, 272)

    def pick(name, k, minus=0, rows=128):
        return A(name, 144 * minus + 15 - k, 144 * minus + 143 - k, rows=rows)

    def slack(t, j, k):
        return A("slb", (t * 3 + j) * 128 + k, (t * 3 + j) * 128 + 128, 16, rows=8)

    def ends(name, c, lo=0, hi=128):
        return A(name, c * 2048 + 16 * lo + 15, c * 2048 + 16 * hi, 16)

    def col(name, k, c0, c1):
        return A(name, c0 * 2048 + 16 * k + 15, c1 * 2048, 256)

    def piece(t, w):
        onv = w[0] == "v"
        w = w[1:] if onv else w
        n = min([w.find(x) for x in "0123" if x in w] + [len(w)])
        kind, c, h = w[:n], int(w[n:n + 1] or 0), w[n + 1:]
        lo, hi = half(h)
        i = t * NL + c

        def H(name, base=0, rows=128):
            return A(name, base + lo, base + hi, rows=rows)

        if kind == "_":
            jobs.append(lambda: None)
        elif kind in ("GA", "GS"):
            own = kind == "GA"
            out = W("gA" if own else "gS", c * 2048 + lo * 16, c * 2048 + hi * 16)
            (vgather if onv else sgather)(out, W("tab"), W("L" if own else "Lr", i * 128 + lo, i * 128 + hi))
        elif kind in ("YA", "YS", "MA", "MS"):
            out, src = [A(n, c * 2048 + lo * 16, c * 2048 + hi * 16) for n in (kind, "g" + kind[1])]
            if kind[0] == "Y":
                scan(out, A("mx", lo * 16, hi * 16), src, op.mult, op.max)
            else:
                scan(out, A("mn", lo * 16, hi * 16), src, op.max, op.min)
        elif kind == "U":
            mm(H("pU"), [(A("Wh"), ends("YA", c, lo, hi)), (A("Wl"), ends("YA", c, lo, hi))])
        elif kind == "e":
            y0, m0 = ends("YA", 0, lo, hi), ends("MA", 0, lo, hi)
            terms = [(Bb, y0), (Bbn, m0)]
            if c == 1:
                terms = terms + terms
            else:
                terms += [(Bb, ends("YA", 1, lo, hi)), (Bbn, ends("MA", 1, lo, hi)), (Bb, H("hx"))]
            terms += 2 * [(A("B8", rows=8), H("slb", (t * 3 + c - 1) * 128, 8))] + [(A("B8", rows=8), H("one", 0, 8))]
            mm(H("pD"), terms, True, False)
        elif kind == "D":
            mm(H("pD"), 2 * [(Bbn, ends("YA", c, lo, hi))] + 2 * [(Bb, ends("MA", c, lo, hi))], False, True)
        elif kind == "H":
            act(A("sg"), A("pD", 0, 128), f=fn.Sign)
            mm(A("pX", 128, 256), [(Ip, ends("YA", 1)), (In, ends("MA", 1)), (In, ends("YA", 0)), (Ip, ends("MA", 0))])
        elif kind == "h":
            tt(A("hx"), A("pX", 128, 256), A("sg"), op.mult)
        elif kind == "B":
            if t == 0:
                act(A("Wh"), Bb, A("wf", 0, 1))
                act(A("Wl"), Bb, A("wf", 1, 2))
                for name in ("-k", "32k", "lift"):
                    act(col_[name], col_["k"], COLS[name][0], COLS[name][1])
                act(A("dm"), A("rowx"), bias=col_["-k"], f=fn.Sign)
                act(A("dm"), A("dm"), DG)
                act(A("dm", 15, 128, 16), A("dm", 15, 128, 16), bias=-18 * DG)
        elif kind == "G":
            if t == 0:
                select(A("I2"), A("one"), [[0, 2], [-1, 144]], op.is_equal, 0, 1)
                iota(A("Er"), [[0, RO * 48]], 0, 0)
                iota(A("cat", 48, 64), [[0, 16]], 0, 0)
        elif kind == "T":
            if t + 1 < RO:
                cp(A("slb", 384 * t + 384, 384 * t + 768, rows=8), A("slI", 384 * t + 384, 384 * t + 768, rows=8))
        elif kind in ("S", "SS"):
            u = t + (kind == "SS")
            if u < RO and (kind == "SS" or t == 0):
                if kind == "S":
                    act(A("Zw"), A("Z2", 0, 144), A("wf", 2, 3))
                    act(A("cK"), A("cKi"), bias=col_["32k"], f=fn.Identity)
                for j in range(2):
                    mm(A("pY", 32 + 8 * j, 40 + 8 * j), [(pick("Z8", k, 1 - j, 8), slack(u, j, k)) for k in range(16)])
                for d in range(2):
                    act(A("a8", 32 * u + d, 32 * u + 32, 2), A("pY", 32, 48))
        elif kind == "K":
            if t > 0:
                ts(A("kf", 0, 1), A("kq", 1, 2), 64.0, col_["613k"], op.mult, op.add)
        elif kind == "Q":
            if t > 0:
                if onv:
                    ts(A("kf", 1, 3), A("kf", 5, 7), A("kf", 0, 1), None, op.add)
                else:
                    act(A("kf", 1, 3), A("kf", 5, 7), bias=A("kf", 0, 1), f=fn.Identity)
        elif kind == "P":
            if c == 0:
                ts(A("NW", 0, 128), A("L", i * 128, i * 128 + 128), 64.0, None, op.mult)
            else:
                cp(H("pV"), H("L", i * 128))
        elif kind == "C":
            cp(H("Ui"), H("pU"))
            ts(H("ua"), H("Ui"), 4095, None, op.bitwise_and)
            if c == 0:
                tt(H("P"), H("ua"), H("NW"), op.mult)
                ts(H("pV", 128), H("P"), 1.0 / 64, A("kf", 0, 1), op.mult, op.add)
            else:
                tt(H("P"), H("ua"), H("pV"), op.mult)
                tt(H("X"), H("P"), H("pD"), op.min)
                ts(H("pV", 128), H("X"), A("kf", c, c + 1), 64.0 * 77 - 2097152.0, op.add, op.max)
            tt(H("Qi"), H("pV", 128), H("NW", c * 128), op.add)
            ts(H("NW", (c + 1) * 128), H("Qi"), 4095 * 64, None, op.bitwise_and)
            ts(H("L", (i + 1) * 128), H("NW", (c + 1) * 128), 1.0 / 64, None, op.mult)
        elif kind == "L":
            send_list(t, c, h)
        elif kind == "N":
            mm(A("pC", 0, 24), [(pick("Z2", k), col("YA", k, 0, 3)) for k in range(16)]
               + [(pick("Z2", k, 1), col("MA", k, 0, 3)) for k in range(16)])
        elif kind == "E":
            mm(A("pX", 80, 88), [(pick("Z8", k, 1, 8), slack(t, 2, k)) for k in range(16)]
               + [(pick("Z2", k), col("YA", k, 3, 4)) for k in range(16)], True, False)
        elif kind == "EE":
            mm(A("pX", 80, 88), [(pick("Z2", k, 1), col("MA", k, 3, 4)) for k in range(16)], False, True)
        elif kind == "i":
            (cp if onv else act)(A("cat", 0, 48, 2), A("pC", 0, 24))
        elif kind == "ii":
            for d in range(2):
                act(A("e3", d, 16, 2), A("pX", 80, 88))
        elif kind == "I":
            n0, m0, d1, t1, m1, s2 = [W("dl", 16 * n, 16 * n + 16) for n in (0, 3, 4, 5, 6, 8)]
            a0, a1 = [A("a8", (t * 2 + j) * 16, (t * 2 + j) * 16 + 16) for j in range(2)]
            tt(A("cat", 1, 48, 2), A("pC", 0, 24), A("Eq", t * 48, t * 48 + 24), op.add)
            gadd(W("dl", 0, 48), W("cat", 0, 16), W("off", 0, 3), W("cat", 16, 64), op.subtract)
            tt(A("HD", 0, 16), n0, a0, op.is_ge)
            tt(m0, n0, A("HD", 0, 16), op.mult)
            gadd(W("dl", 64, 96), m0, W("off", 0, 2), W("dl", 16, 48), op.subtract)
            tt(A("HD", 16, 32), d1, a1, op.is_le)
            tt(m1, d1, A("HD", 16, 32), op.mult)
            tt(s2, t1, m1, op.subtract)
            tt(A("HD", 0, 32, 2), A("HD", 0, 32, 2), A("HD", 1, 32, 2), op.is_equal)
            gadd(W("HD", 16, 32), W("HD", 0, 16), W("off", 4, 5), W("HD", 16, 32), op.mult)
        elif kind == "II":
            tt(A("dl", 112, 128), A("dl", 128, 144), A("e3"), op.add)
        elif kind == "u":
            mm(A("pZ", 0, 32), [(pick("Zw", k), col("YA", k, 0, 4)) for k in range(16)])
        elif kind == "Ja":
            cp(A("Ki", 0, 32), A("pZ", 0, 32))
            ts(A("Ki", 32, 64), A("Ki", 0, 32), 31, None, op.bitwise_and)
            gadd(W("K"), W("Ki", 32, 64), W("off", 6, 8), W("cK"))
        elif kind == "F":
            mm(A("pY", 0, 24), [(pick("Z2", k), col("YS", k, 0, 3)) for k in range(16)], True, False)
        elif kind == "FF":
            mm(A("pY", 0, 24), [(pick("Z2", k, 1), col("MS", k, 0, 3)) for k in range(16)], False, True)
        elif kind == "R":
            (cp if onv else act)(A("Er", t * 48, t * 48 + 24), A("pY", 0, 24))
            send_reply(t, 0, 24, "e%d" % (2 * t))
        elif kind == "W":
            mm(H("pW"), [(Bb, ends("YS", 3, lo, hi))], True, False)
        elif kind == "w":
            mm(H("pW"), [(Bbn, ends("MS", 3, lo, hi))], False, True)
        elif kind == "r":
            scan(H("dg"), H("pW"), H("dm"), op.max, op.add)
            ts(A("Er", t * 48 + 33 + lo // 8, t * 48 + 32 + hi // 8, 2), A("dg", lo + 15, hi, 16), col_["lift"], -1.0 / BIG,
               op.add, op.mult)
            send_reply(t, 32 + lo // 8, 32 + hi // 8, "e%d%s" % (2 * t + 1, h))
        elif kind == "Jb":
            tt(A("cf", 0, 32), A("HD", 0, 32), A("K"), op.mult)
            tt(A("cf", 32, 40), A("K", 0, 16, 2), A("cf", 1, 16, 2), op.max)
            tt(A("cf", 40, 48), A("cf", 32, 40), A("cf", 17, 32, 2), op.max)
        elif kind == "Z":
            last = t == RO - 1
            n = t * 48 + 32
            tt(A("HD", 32, 48), A("dl", 112, 128), A("Eq", n, n + 16), op.is_le)
            tt(A("rt", 0, 8), A("HD", 33, 48, 2), A("cf", 16, 32, 2), op.mult)
            if not last:
                tt(A("rt", 8, 16), A("HD", 32, 48, 2), A("HD", 33, 48, 2), op.is_equal)
            tt(A("ci", 0, 8), A("rt", 0, 8), A("cf", 40, 48), op.max)
            if not last:
                tt(A("r3"), A("rt", 8, 16), A("HD", 16, 32, 2), op.mult)
                mm(A("pX", 256, 257), [(neg, A("r3", n, n + 1)) for n in range(8)])
            ts(A("ci", 8, 16), A("ci", 0, 8), 5, None, op.arith_shift_right)
            ts(A("ci", 16, 24), A("ci", 0, 8), 2047 if last else 4095, None, op.bitwise_and)
            cp(A("o13"), A("ci", 8, 24))
            o1 = W("o13", 0, 8)

            def o3(a, b):
                return W("o13", 8 + a // 16, 8 + b // 16)

            def mean(a, b):
                gadd(W("sm", a, b), W("YA"), W("o2", a // 16, b // 16), W("old", a, b))

            def down(a, b):
                ts(A("sn", a, b), A("sm", a, b), 1, None, op.arith_shift_right)

            def put(a, b):
                scatter(W("tab", 32 * a, 32 * b), o3(a, b), W("sn", a, b))

            if not last:
                nxt = (t + 1) * NL * 128
                sgather(W("old"), W("tab"), o3(0, 128), 0.5, -0.25)
                ts(A("o2"), o1, 16.0, 15.0, op.mult, op.add)
                sgather(W("yh"), W("YA"), W("o2"), 0.5)
                ts(W("L", nxt, nxt + 128), W("NW"), 1.0 / 64, None, op.mult, off=o1)
                send_list(t + 1, 0)
                cp(A("kq", 0, 1), A("pX", 256, 257))
                tt(A("sn"), A("old"), A("yh"), op.add)
                ts(A("kq", 1, 2), A("kq", 0, 1), 31, None, op.bitwise_and)
                put(0, 128)
            else:
                for a, b in ((0, 64), (64, 128)):
                    sgather(W("old", a, b), W("tab", 32 * a, 32 * b), o3(a, b))
                ts(A("o2"), o1, 16.0, 15.0, op.mult, op.add)
                ts(W("fin"), W("NW"), 1.0 / 64, None, op.mult, off=o1)
                dma("y", ext(T.yc[:, :]), W("fin"), "st2")
                mean(0, 64)
                mean(64, 128)
                down(0, 64)
                down(64, 128)
                put(0, 64)
                dma("y", ext(T.yx[:, 0:2048]), W("tab", 0, 2048), "st0")
                put(64, 128)
                dma("s", ext(T.yx[:, 2048:4096]), W("tab", 2048, 4096), "st1")

    issue(taken())
    for t in range(RO):
        held = {}
        for w in ORDER.split():
            if ":" in w:
                x, n = w.split(":")
                if x not in held:
                    piece(t, x)
                    held[x] = taken()
                issue(held[x][int(n[0], 36):int(n[1], 36)])
                continue
            chains = []
            for x in w.split("+"):
                for y in x.split("."):
                    piece(t, y)
                chains.append(taken())
            issue(*chains)

    for q in "vspg":
        g.wait_ge(T.sem["q" + q], cnt[q])
    g.wait_ge(T.sem.sent, sends[0])
    for s in ("ld0", "ld1", "ld2", "ld3", "st0", "st1", "st2"):
        g.wait_ge(T.sem[s], 16)
